import numpy as np
import ml_dtypes


def mxq(x, axis, fmt="e4m3"):
    dtype, down = {"e4m3": (ml_dtypes.float8_e4m3fn, 7), "e5m2": (ml_dtypes.float8_e5m2, 14)}[fmt]
    v = np.moveaxis(np.asarray(x, np.float32).astype(ml_dtypes.bfloat16).astype(np.float64), axis, -1)
    blocks = v.reshape(v.shape[:-1] + (-1, 32))
    amax = np.abs(blocks).max(-1, keepdims=True)
    byte = np.maximum(np.where(amax > 0, np.frexp(amax)[1] - 1 + 127, 0) - down, 1)
    scale = np.exp2(byte - 127.0)
    codes = (blocks / scale).astype(np.float32).astype(dtype).astype(np.float64)
    return np.moveaxis((codes * scale).reshape(v.shape), -1, axis)


WIDE = False


def mx_kscale(k):
    if not WIDE:
        return np.ones(k)
    levels = np.array([10, -10, 5, -5, 0])
    if k % 512:
        return np.exp2(np.random.permutation(np.resize(levels, k // 32))).repeat(32)
    a = np.empty((k // 512, 16))
    for p in range(k // 512):
        a[p, :8] = np.random.permutation(np.resize(levels, 8))
        for g in range(8):
            far = levels[np.abs(levels - a[p, g]) >= 10]
            a[p, g + 8] = far[np.random.randint(len(far))]
    return np.exp2(a.ravel()).repeat(32)


BF16 = ml_dtypes.bfloat16


def bf(x):
    return np.asarray(x, np.float32).astype(BF16)


def f64(x):
    return np.asarray(x).astype(np.float64)


E2M1 = np.array([0.0, 0.5, 1.0, 1.5, 2.0, 3.0, 4.0, 6.0, -0.0, -0.5, -1.0, -1.5, -2.0, -3.0, -4.0, -6.0])


def pack_weight(w, fmt):
    k, n = w.shape
    w = f64(bf(w)).reshape(k // 32, 32, n)
    amax = np.abs(w).max(1)
    if fmt == "e4m3":
        byte = np.frexp(amax)[1] - 1 + 127 - 7
    else:
        mant, ex = np.frexp(amax / 6.0)
        byte = np.where(mant > 0.5, ex, ex - 1) + 127
    byte = np.clip(np.where(amax > 0, byte, 1), 1, 254)
    scaled = (w * np.exp2(127.0 - byte)[:, None, :]).reshape(k, n).astype(np.float32)
    by_word = np.ascontiguousarray(scaled.reshape(k // 512, 128, 4, n).transpose(0, 1, 3, 2))
    if fmt == "e4m3":
        words = by_word.astype(ml_dtypes.float8_e4m3fn).view(np.uint8)
    else:
        c = by_word.astype(ml_dtypes.float4_e2m1fn).view(np.uint8) & 0xF
        words = c[..., 0::2] | (c[..., 1::2] << 4)
    return np.ascontiguousarray(words), np.ascontiguousarray(byte.astype(np.uint8).reshape(k // 512, 16, n))


def unpack_weight(words, scales, fmt):
    g, p, n, _ = words.shape
    if fmt == "e4m3":
        vals = np.ascontiguousarray(words).view(ml_dtypes.float8_e4m3fn).astype(np.float64)
    else:
        nib = np.empty((g, p, n, 4), np.uint8)
        nib[..., 0::2] = words & 0xF
        nib[..., 1::2] = words >> 4
        vals = E2M1[nib]
    vals = vals * np.repeat(np.exp2(scales.astype(np.float64) - 127.0), 8, axis=1)[..., None]
    return vals.transpose(0, 1, 3, 2).reshape(g * 512, n)
def pack4(w):
    words, scales = pack_weight(w, "e2m1")
    return words.reshape(words.shape[0], 128, -1), scales


def unpack4(words, scales):
    return unpack_weight(words.reshape(words.shape[0], 128, -1, 2), scales, "e2m1")


N, D, E, G = 1024, 1024, 1024, 3


def gained_product(left, right, p_row, q_row):
    return mxq(left * p_row[None, :], 1, "e4m3") @ mxq(q_row[:, None] * right, 0, "e4m3")


def mod_relu(z, b):
    return np.sign(z) * np.maximum(np.abs(z) + b[None, :], 0.0)


def draw0():
    cx = mx_kscale(E)
    c = np.stack([mx_kscale(D) for _ in range(G)])
    h = np.random.standard_normal((N, D))
    x = np.random.standard_normal((N, E)) * cx[None, :]
    a = np.random.standard_normal((D, D)) / np.sqrt(D)
    t = np.random.standard_normal((E, D)) / np.sqrt(E) / cx[:, None]
    t_words, t_scales = pack4(t)
    p = (1.0 + 0.2 * np.random.standard_normal((G, D))) * c
    q = (1.0 + 0.2 * np.random.standard_normal((G, D))) / c
    b = np.random.uniform(-0.5, -0.1, D)
    return {"h": bf(h), "x": bf(x), "a": bf(a), "t_words": t_words, "t_scales": t_scales, "p": bf(p), "q": bf(q), "b": bf(b)}


def core(h, x, a, t_words, t_scales, p, q, b):
    h, x, a, p, q, b = f64(h), f64(x), f64(a), f64(p), f64(q), f64(b)
    s = a - a.T
    k1 = gained_product(h, s, p[0], q[0])
    s2 = gained_product(s, s, p[1], q[1])
    r = s / 2.0 + s2 / 6.0
    k23 = gained_product(k1, r, p[2], q[2])
    u = mxq(x, 1, "e4m3") @ unpack4(t_words, t_scales)
    z = h + k1 + k23 + u
    return mod_relu(z, b)


def e4m3fn_bytes(y):
    return np.clip(np.asarray(y, np.float64), -448.0, 448.0).astype(np.float32).astype(ml_dtypes.float8_e4m3fn).view(np.uint8)


def e4m3fn_values(b):
    return np.asarray(b, np.uint8).view(ml_dtypes.float8_e4m3fn).astype(np.float64)


def setup_inputs():
    d = draw0()
    x0 = np.asarray(d['x']).astype(np.float64)
    s = (np.max(np.abs(x0), axis=(0,), keepdims=True) / 448.0).astype(np.float32)
    out = {}
    for k, v in d.items():
        if k == 'x':
            out['x_bytes'] = e4m3fn_bytes(x0 / s.astype(np.float64))
            out['x_scale'] = s
        else:
            out[k] = v
    return out


def reference(h, x_bytes, x_scale, a, t_words, t_scales, p, q, b):
    return core(h, e4m3fn_values(x_bytes) * x_scale.astype(np.float64), a, t_words, t_scales, p, q, b)

@@ -1,0 +1,286 @@
+from contextlib import ExitStack
+
+import concourse.mybir as mybir
+from concourse.masks import make_identity
+
+F32 = mybir.dt.float32
+BF16 = mybir.dt.bfloat16
+U32 = mybir.dt.uint32
+I32 = mybir.dt.int32
+U8 = mybir.dt.uint8
+F8 = mybir.dt.float8_e4m3fn
+E4X4 = mybir.dt.float8_e4m3fn_x4
+E2X4 = mybir.dt.float4_e2m1fn_x4
+ALU = mybir.AluOpType
+ACT = mybir.ActivationFunctionType
+
+P = 128
+N = 1024
+D = 1024
+J = N // P
+G = 2
+T = 4
+H = 512
+FLOPS = 4 * 2 * N * D * D
+
+
+def tile_skewexptaylorrecurrentstep_w4_kernel(tc, h, x_bytes, x_scale, a, t_words, t_scales, p, q, b, out):
+    nc = tc.nc
+    with ExitStack() as ctx:
+        keep = ctx.enter_context(tc.tile_pool(name="keep", bufs=1))
+        work = ctx.enter_context(tc.tile_pool(name="work", bufs=2))
+        roll = ctx.enter_context(tc.tile_pool(name="roll", bufs=3))
+        psum_s = ctx.enter_context(tc.psum_pool(name="psum_s", bufs=3))
+        psum_t = ctx.enter_context(tc.psum_pool(name="psum_t", bufs=2))
+        psum_a = ctx.enter_context(tc.psum_pool(name="psum_a", bufs=3))
+
+        gq = keep.tile([P, 6, T], BF16, name="gq")
+        nc.scalar.dma_start(out=gq[:], in_=q.rearrange("i k -> (i k)").rearrange("(a p t) -> p a t", p=P, t=T))
+        gp = keep.tile([P, G, T], BF16, name="gp")
+        nc.scalar.dma_start(out=gp[:], in_=p[1, :].rearrange("(g p t) -> p g t", p=P, t=T))
+
+        ak = {}
+        ar = {}
+        hrow = keep.tile([P, J, D], BF16, name="hrow")
+
+        def load_a(c, g):
+            t1 = roll.tile([P, T, H], BF16, name="ak", tag="ak")
+            nc.sync.dma_start(out=t1[:], in_=a[g * H:(g + 1) * H, c * H:(c + 1) * H].rearrange("(p t) n -> p t n", t=T))
+            t2 = roll.tile([P, 4, H], BF16, name="ar", tag="ar")
+            nc.sync.dma_start(out=t2[:], in_=a[c * H:(c + 1) * H, g * H:(g + 1) * H].rearrange("(j p) k -> p j k", p=P))
+            ak[c, g] = t1
+            ar[c, g] = t2
+
+        def load_h(j0, j1):
+            nc.sync.dma_start(out=hrow[:, j0:j1, :], in_=h[j0 * P:j1 * P, :].rearrange("(j p) k -> p j k", p=P))
+
+        load_a(0, 0)
+        pb0 = keep.tile([P, D], BF16, name="pb0")
+        nc.sync.dma_start(out=pb0[:], in_=p[0, :].partition_broadcast(P))
+        load_h(0, 2)
+        load_h(2, 4)
+        load_a(0, 1)
+        load_h(4, 8)
+        pb2 = keep.tile([P, D], BF16, name="pb2")
+        nc.sync.dma_start(out=pb2[:], in_=p[2, :].partition_broadcast(P))
+        load_a(1, 0)
+        load_a(1, 1)
+        xs = keep.tile([P, D], F32, name="xs")
+        nc.sync.dma_start(out=xs[:], in_=x_scale.rearrange("o k -> (o k)").partition_broadcast(P))
+        xbs = []
+        for jp in range(4):
+            xb = roll.tile([P, 2, D], U8, name="xb", tag="xb", bufs=2)
+            nc.sync.dma_start(out=xb[:], in_=x_bytes[2 * jp * P:(2 * jp + 2) * P, :].rearrange("(j p) k -> p j k", p=P))
+            xbs.append(xb)
+        tw = keep.tile([P, G, 2 * D], U8, name="tw", align_bytes=64)
+        nc.sync.dma_start(out=tw[:], in_=t_words.rearrange("g p n -> p g n"))
+        ts = keep.tile([P, G, D], U8, name="ts", align_bytes=64)
+        nc.gpsimd.memset(ts[:].rearrange("p g n -> p (g n)").bitcast(I32), 0)
+        for quad in range(4):
+            nc.sync.dma_start(
+                out=ts[32 * quad:32 * quad + 4, :, :].bitcast(I32),
+                in_=t_scales[:, 4 * quad:4 * quad + 4, :].rearrange("g r n -> r g n").bitcast(I32),
+            )
+        bb = keep.tile([P, D], BF16, name="bb")
+        nc.sync.dma_start(out=bb[:], in_=b.partition_broadcast(P))
+
+        ident = keep.tile([P, P], BF16, name="ident")
+        make_identity(nc, ident[:])
+        identf = keep.tile([P, P], F32, name="identf")
+        make_identity(nc, identf[:])
+        negid = keep.tile([P, P], BF16, name="negid")
+        nc.vector.tensor_scalar(out=negid[:], in0=ident[:], scalar1=-1.0, scalar2=None, op0=ALU.mult)
+        fq = keep.tile([P, 6, T], F32, name="fq")
+        nc.vector.tensor_copy(out=fq[:], in_=gq[:])
+        fp = keep.tile([P, G, T], F32, name="fp")
+        nc.vector.tensor_scalar(out=fp[:], in0=gp[:], scalar1=-1.0, scalar2=None, op0=ALU.mult)
+        fq2h = keep.tile([P, G, T], F32, name="fq2h")
+        nc.vector.tensor_scalar(out=fq2h[:], in0=gq[:, 4:6, :], scalar1=0.5, scalar2=None, op0=ALU.mult)
+        fq2s = keep.tile([P, G, T], F32, name="fq2s")
+        nc.vector.tensor_scalar(out=fq2s[:], in0=gq[:, 4:6, :], scalar1=1.0 / 6.0, scalar2=None, op0=ALU.mult)
+
+        def operand(name):
+            c = keep.tile([P, G, D], U32, name=name + "_c", align_bytes=64)
+            s = keep.tile([P, G, D], U8, name=name + "_s", align_bytes=64)
+            return c, s
+
+        def left(name):
+            c = keep.tile([P, J, G, P], U32, name=name + "_c", align_bytes=64)
+            s = keep.tile([P, J, G, P], U8, name=name + "_s", align_bytes=64)
+            return c, s
+
+        q0s, q1s, p1s, q2r = operand("q0s"), operand("q1s"), operand("p1s"), operand("q2r")
+        hp, xp = left("hp"), left("xp")
+        kp_c = keep.tile([P, G, J, P], U32, name="kp_c", align_bytes=64)
+        kp_s = keep.tile([P, G, J, P], U8, name="kp_s", align_bytes=64)
+        sq = keep.tile([P, G, 2, T, H], F32, name="sq")
+
+        def turn(row, dst, jj, il):
+            words = row.bitcast(F32)
+            bank = psum_t.tile([P, 4, P], F32, name="bank")
+            for g in range(G):
+                for u in range(2):
+                    nc.tensor.transpose(bank[:, 2 * g + u, :], words[:, 256 * g + u:256 * (g + 1):2], identf[:])
+            nc.scalar.copy(
+                out=il[:, jj, :, :, :].rearrange("p g n t -> p g (n t)").bitcast(F32).rearrange("p g (n u) -> p g n u", u=2),
+                in_=bank[:].rearrange("p (g u) n -> p g n u", u=2),
+            )
+
+        def do_left(jp, dst, make_row):
+            il = work.tile([P, 2, G, P, T], BF16, name="lil", align_bytes=64)
+            for jj in range(2):
+                row = work.tile([P, D], BF16, name="lrow", align_bytes=64)
+                make_row(2 * jp + jj, row)
+                turn(row[:], dst, jj, il)
+            nc.vector.quantize_mx(
+                out=dst[0][:, 2 * jp:2 * jp + 2, :, :].rearrange("p j g n -> p (j g n)").bitcast(E4X4),
+                scales=dst[1][:, 2 * jp:2 * jp + 2, :, :].rearrange("p j g n -> p (j g n)"),
+                in_=il[:].rearrange("p j g n t -> p (j g n t)"),
+            )
+
+        def h_row(j, row):
+            nc.vector.tensor_tensor(out=row[:], in0=hrow[:, j, :], in1=pb0[:], op=ALU.mult)
+
+        def x_row(j, row):
+            nc.vector.tensor_tensor(out=row[:], in0=xbs[j // 2][:, j % 2, :].bitcast(F8), in1=xs[:], op=ALU.mult)
+
+        def quant_right(op, g, c, il):
+            nc.vector.quantize_mx(
+                out=op[0][:, g, c * H:(c + 1) * H].bitcast(E4X4),
+                scales=op[1][:, g, c * H:(c + 1) * H],
+                in_=il[:].rearrange("p n t -> p (n t)"),
+            )
+
+        def s_group(c, g):
+            pl = {}
+            for nm in ("p1", "q0", "q1"):
+                pl[nm] = work.tile([P, T, H], BF16, name="pl", tag="pl", bufs=4)
+            for t in range(T):
+                bank = psum_s.tile([P, H], F32, name="sbank")
+                nc.tensor.matmul(bank[:], lhsT=ident[:], rhs=ak[c, g][:, t, :], start=True, stop=False)
+                for jj in range(4):
+                    nc.tensor.matmul(bank[:, jj * P:(jj + 1) * P], lhsT=ar[c, g][:, jj, t::T], rhs=negid[:], start=False, stop=(jj == 3))
+                nc.scalar.activation(out=pl["p1"][:, t, :], in_=bank[:], func=ACT.Copy, scale=fp[:, g, t:t + 1])
+                nc.scalar.activation(out=pl["q1"][:, t, :], in_=bank[:], func=ACT.Copy, scale=fq[:, 2 + g, t:t + 1])
+                nc.scalar.activation(out=pl["q0"][:, t, :], in_=bank[:], func=ACT.Copy, scale=fq[:, g, t:t + 1])
+                nc.scalar.activation(out=sq[:, g, c, t, :], in_=bank[:], func=ACT.Copy, scale=fq2h[:, g, t:t + 1])
+            ils = {}
+            for nm in ("p1", "q0", "q1"):
+                il = work.tile([P, H, T], BF16, name="il", tag="il", bufs=3, align_bytes=64)
+                if nm == "p1":
+                    nc.vector.tensor_copy(
+                        out=il[:].rearrange("p (tt m) t -> p tt m t", tt=T),
+                        in_=pl[nm][:].rearrange("p t (m tt) -> p tt m t", tt=T),
+                    )
+                else:
+                    nc.vector.tensor_copy(
+                        out=il[:].rearrange("p (c i) t -> p c t i", i=4),
+                        in_=pl[nm][:].rearrange("p t (c i) -> p c t i", i=4),
+                    )
+                ils[nm] = il
+            quant_right(p1s, g, c, ils["p1"])
+            quant_right(q0s, g, c, ils["q0"])
+            quant_right(q1s, g, c, ils["q1"])
+
+        def mx(acc, lc, ls, rc, rs, first, last, fp4=False):
+            nc.tensor.matmul_mx(
+                out=acc,
+                lhsT=lc.bitcast(E4X4), lhsT_scale=ls,
+                rhs=rc.bitcast(E2X4 if fp4 else E4X4), rhs_scale=rs,
+                start=first, stop=last,
+            )
+
+        def right(op, g, c):
+            return op[0][:, g, c * H:(c + 1) * H], op[1][:, g, c * H:(c + 1) * H]
+
+        def k_pair(c, jp):
+            il = work.tile([P, 2, P, T], BF16, name="kil", align_bytes=64)
+            bank = psum_t.tile([P, 4, P], F32, name="bank")
+            for jj in range(2):
+                j = 2 * jp + jj
+                acc = psum_a.tile([P, H], F32, name="acc")
+                for g in range(G):
+                    rc, rs = right(q0s, g, c)
+                    mx(acc[:], hp[0][:, j, g, :], hp[1][:, j, g, :], rc, rs, g == 0, g == 1)
+                row = work.tile([P, H], BF16, name="krow", align_bytes=64)
+                nc.vector.tensor_tensor(out=row[:], in0=acc[:], in1=pb2[:, c * H:(c + 1) * H], op=ALU.mult)
+                words = row[:].bitcast(F32)
+                for u in range(2):
+                    nc.tensor.transpose(bank[:, 2 * jj + u, :], words[:, u::2], identf[:])
+            nc.scalar.copy(
+                out=il[:].rearrange("p j n t -> p j (n t)").bitcast(F32).rearrange("p j (n u) -> p j n u", u=2),
+                in_=bank[:].rearrange("p (j u) n -> p j n u", u=2),
+            )
+            nc.vector.quantize_mx(
+                out=kp_c[:, c, 2 * jp:2 * jp + 2, :].rearrange("p j n -> p (j n)").bitcast(E4X4),
+                scales=kp_s[:, c, 2 * jp:2 * jp + 2, :].rearrange("p j n -> p (j n)"),
+                in_=il[:].rearrange("p j n t -> p (j n t)"),
+            )
+
+        def r_group(c, gm):
+            rq = work.tile([P, T, H], F32, name="rq")
+            for t in range(T):
+                acc = psum_a.tile([P, H], F32, name="acc")
+                m0 = gm * H + t * P
+                for g in range(G):
+                    rc, rs = right(q1s, g, c)
+                    mx(acc[:], p1s[0][:, g, m0:m0 + P], p1s[1][:, g, m0:m0 + P], rc, rs, g == 0, g == 1)
+                nc.scalar.activation(out=rq[:, t, :], in_=acc[:], func=ACT.Copy, scale=fq2s[:, gm, t:t + 1])
+            il = work.tile([P, H, T], BF16, name="il", tag="il", bufs=3, align_bytes=64)
+            nc.vector.tensor_tensor(
+                out=il[:],
+                in0=rq[:].rearrange("p t n -> p n t"),
+                in1=sq[:, gm, c, :, :].rearrange("p t n -> p n t"),
+                op=ALU.add,
+            )
+            quant_right(q2r, gm, c, il)
+
+        def z_pair(c, jp):
+            cs = slice(c * H, (c + 1) * H)
+            z = roll.tile([P, 2, H], F32, name="z", tag="ak")
+            for jj in range(2):
+                j = 2 * jp + jj
+                acc = psum_a.tile([P, H], F32, name="acc")
+                for g in range(G):
+                    rc, rs = right(q0s, g, c)
+                    mx(acc[:], hp[0][:, j, g, :], hp[1][:, j, g, :], rc, rs, g == 0, False)
+                for g in range(G):
+                    mx(acc[:], xp[0][:, j, g, :], xp[1][:, j, g, :], tw[:, g, 2 * c * H:2 * (c + 1) * H], ts[:, g, cs], False, False, True)
+                for g in range(G):
+                    rc, rs = right(q2r, g, c)
+                    mx(acc[:], kp_c[:, g, j, :], kp_s[:, g, j, :], rc, rs, False, g == 1)
+                nc.vector.tensor_tensor(out=z[:, jj, :], in0=acc[:], in1=hrow[:, j, cs], op=ALU.add)
+            za = roll.tile([P, 2, H], F32, name="za", tag="ar")
+            nc.scalar.activation(out=za[:], in_=z[:], func=ACT.Abs)
+            sg = roll.tile([P, 2, H], BF16, name="sg")
+            nc.scalar.activation(out=sg[:], in_=z[:], func=ACT.Sign)
+            nc.vector.tensor_tensor(out=za[:], in0=za[:], in1=bb[:, cs].unsqueeze(1).to_broadcast([P, 2, H]), op=ALU.add)
+            nc.vector.scalar_tensor_tensor(out=za[:], in0=za[:], scalar=0.0, in1=sg[:], op0=ALU.max, op1=ALU.mult)
+            nc.sync.dma_start(out=out[2 * jp * P:(2 * jp + 2) * P, cs].rearrange("(j p) d -> p j d", p=P), in_=za[:])
+
+        s_group(0, 0)
+        do_left(0, hp, h_row)
+        do_left(1, hp, h_row)
+        s_group(0, 1)
+        do_left(2, hp, h_row)
+        do_left(3, hp, h_row)
+        s_group(1, 0)
+        for jp in range(4):
+            k_pair(0, jp)
+        s_group(1, 1)
+        do_left(0, xp, x_row)
+        do_left(1, xp, x_row)
+        r_group(0, 0)
+        r_group(0, 1)
+        do_left(2, xp, x_row)
+        do_left(3, xp, x_row)
+        for jp in range(4):
+            k_pair(1, jp)
+        r_group(1, 0)
+        z_pair(0, 0)
+        z_pair(0, 1)
+        r_group(1, 1)
+        z_pair(0, 2)
+        z_pair(0, 3)
+        for jp in range(4):
+            z_pair(1, jp)

@@ -21,6 +21,317 @@ J = N // P
 G = 2
 T = 4
 H = 512
+WIDE = ((0, 0),)
+ORDER = [
+    ("smulv", "p0"),
+    ("smulv", "x1"),
+    ("vcopy", "p0"),
+    ("smulv", "x0"),
+    ("vcopy", "x1"),
+    ("row", "h", 0),
+    ("vcopy", "x0"),
+    ("wmul", 0, 0, 0),
+    ("row", "h", 1),
+    ("turn", "h", 0),
+    ("whalf", 0, 0, 0),
+    ("wgain", "q0", 0, 0, 0),
+    ("wmul", 0, 0, 2),
+    ("lcp", "h", 0),
+    ("wgain", "q1", 0, 0, 0),
+    ("wmul", 0, 0, 3),
+    ("whalf", 0, 0, 2),
+    ("wgain", "q0", 0, 0, 2),
+    ("wmul", 0, 0, 1),
+    ("wgain", "p1", 0, 0, 0),
+    ("whalf", 0, 0, 3),
+    ("turn", "h", 1),
+    ("wgain", "q1", 0, 0, 1),
+    ("whalf", 0, 0, 1),
+    ("wgain", "q1", 0, 0, 3),
+    ("smul", 0, 1, 2),
+    ("lcp", "h", 1),
+    ("wgain", "p1", 0, 0, 1),
+    ("smul", 0, 1, 0),
+    ("lq", "h", 0),
+    ("sscale", 0, 1, 2),
+    ("smul", 0, 1, 1),
+    ("wgain", "q0", 0, 0, 3),
+    ("smul", 0, 1, 3),
+    ("row", "h", 3),
+    ("sscale", 0, 1, 1),
+    ("wgain", "p1", 0, 0, 3),
+    ("wgain", "q0", 0, 0, 1),
+    ("row", "h", 4),
+    ("sscale", 0, 1, 0),
+    ("rq", "q0", 0, 0),
+    ("wgain", "q1", 0, 0, 2),
+    ("row", "h", 5),
+    ("shalf", 0, 1, 3),
+    ("shalf", 0, 1, 1),
+    ("sscale", 0, 1, 3),
+    ("wgain", "p1", 0, 0, 2),
+    ("rq", "q1", 0, 0),
+    ("smul", 1, 0, 2),
+    ("rq", "p1", 0, 0),
+    ("smul", 1, 0, 1),
+    ("shalf", 0, 1, 0),
+    ("lay", "q0", 0, 1),
+    ("smul", 1, 0, 0),
+    ("sscale", 1, 0, 2),
+    ("smul", 1, 1, 0),
+    ("sscale", 1, 0, 0),
+    ("lay", "q1", 0, 1),
+    ("shalf", 0, 1, 2),
+    ("rq", "q0", 0, 1),
+    ("sscale", 1, 0, 1),
+    ("lay", "p1", 0, 1),
+    ("turn", "h", 3),
+    ("kmul", 0, 1),
+    ("sscale", 1, 1, 0),
+    ("smul", 1, 1, 1),
+    ("row", "h", 2),
+    ("kmul", 0, 0),
+    ("krow", 0, 1),
+    ("lcp", "h", 3),
+    ("smulb", 1, 0, 1),
+    ("rq", "q1", 0, 1),
+    ("sscale", 1, 1, 1),
+    ("turn", "h", 4),
+    ("krow", 0, 0),
+    ("smul", 1, 0, 3),
+    ("sscaleb", 1, 0, 1),
+    ("rq", "p1", 0, 1),
+    ("kturn", 0, 0),
+    ("lcp", "h", 4),
+    ("row", "x", 3),
+    ("sscale", 1, 0, 3),
+    ("rmul", 0, 0, 1),
+    ("shalf", 1, 0, 1),
+    ("rmul", 0, 0, 0),
+    ("rscale", 0, 0, 1),
+    ("smulb", 1, 0, 0),
+    ("lay", "q0", 1, 0),
+    ("rscale", 0, 0, 0),
+    ("turn", "h", 2),
+    ("kcp", 0, 0),
+    ("rmul", 0, 0, 3),
+    ("shalf", 1, 0, 0),
+    ("sscaleb", 1, 0, 0),
+    ("rmul", 0, 0, 2),
+    ("kq", 0, 0),
+    ("rscale", 0, 0, 3),
+    ("turn", "h", 5),
+    ("rq", "q0", 1, 0),
+    ("rscale", 0, 0, 2),
+    ("smul", 1, 1, 2),
+    ("lay", "p1", 1, 0),
+    ("lcp", "h", 2),
+    ("smulb", 1, 0, 3),
+    ("lcp", "h", 5),
+    ("turn", "x", 3),
+    ("sscaleb", 1, 0, 3),
+    ("row", "h", 7),
+    ("smulb", 1, 1, 2),
+    ("sscale", 1, 1, 2),
+    ("row", "x", 2),
+    ("smulb", 1, 1, 1),
+    ("smulb", 1, 1, 0),
+    ("sscaleb", 1, 1, 2),
+    ("radd", 0, 0),
+    ("turn", "x", 2),
+    ("sscaleb", 1, 1, 1),
+    ("smulb", 1, 0, 2),
+    ("sscaleb", 1, 1, 0),
+    ("smul", 1, 1, 3),
+    ("shalf", 1, 0, 3),
+    ("sscaleb", 1, 0, 2),
+    ("row", "x", 1),
+    ("smulb", 1, 1, 3),
+    ("shalf", 1, 1, 1),
+    ("sscaleb", 1, 1, 3),
+    ("lay", "q1", 1, 0),
+    ("shalf", 1, 1, 3),
+    ("sscale", 1, 1, 3),
+    ("lq", "h", 1),
+    ("rq", "q1", 1, 0),
+    ("lcp", "x", 2),
+    ("shalf", 1, 0, 2),
+    ("shalf", 1, 1, 0),
+    ("rq", "p1", 1, 0),
+    ("shalf", 1, 1, 2),
+    ("lq", "h", 2),
+    ("lcp", "x", 3),
+    ("rq", "r", 0, 0),
+    ("lay", "q0", 1, 1),
+    ("kmul", 0, 3),
+    ("lq", "x", 1),
+    ("kmul", 0, 2),
+    ("krow", 0, 3),
+    ("kmul", 0, 4),
+    ("krow", 0, 2),
+    ("kmul", 0, 5),
+    ("krow", 0, 4),
+    ("turn", "x", 1),
+    ("lay", "p1", 1, 1),
+    ("rq", "q0", 1, 1),
+    ("kturn", 0, 1),
+    ("turn", "h", 7),
+    ("krow", 0, 5),
+    ("kmul", 1, 1),
+    ("row", "h", 6),
+    ("kmul", 1, 0),
+    ("kcp", 0, 1),
+    ("krow", 1, 1),
+    ("kturn", 0, 2),
+    ("lcp", "x", 1),
+    ("rq", "p1", 1, 1),
+    ("kmul", 1, 2),
+    ("lcp", "h", 7),
+    ("krow", 1, 0),
+    ("rmul", 0, 1, 0),
+    ("kcp", 0, 2),
+    ("kq", 0, 1),
+    ("rmul", 0, 1, 2),
+    ("krow", 1, 2),
+    ("lay", "q1", 1, 1),
+    ("kmul", 1, 3),
+    ("kq", 0, 2),
+    ("row", "x", 0),
+    ("kturn", 1, 0),
+    ("kmul", 1, 5),
+    ("krow", 1, 3),
+    ("rmul", 0, 1, 1),
+    ("rscale", 0, 1, 0),
+    ("krow", 1, 5),
+    ("kmul", 1, 4),
+    ("rscale", 0, 1, 2),
+    ("row", "x", 5),
+    ("kturn", 1, 1),
+    ("kcp", 1, 0),
+    ("turn", "h", 6),
+    ("rscale", 0, 1, 1),
+    ("krow", 1, 4),
+    ("rmul", 0, 1, 3),
+    ("kcp", 1, 1),
+    ("kq", 1, 0),
+    ("kturn", 1, 2),
+    ("row", "x", 6),
+    ("lcp", "h", 6),
+    ("turn", "x", 5),
+    ("rscale", 0, 1, 3),
+    ("turn", "x", 0),
+    ("kq", 1, 1),
+    ("kcp", 1, 2),
+    ("lq", "h", 3),
+    ("turn", "x", 6),
+    ("lcp", "x", 0),
+    ("kq", 1, 2),
+    ("kmul", 1, 6),
+    ("rq", "q1", 1, 1),
+    ("kmul", 1, 7),
+    ("lq", "x", 0),
+    ("rmul", 1, 1, 0),
+    ("krow", 1, 6),
+    ("lcp", "x", 5),
+    ("rmul", 1, 1, 3),
+    ("krow", 1, 7),
+    ("lcp", "x", 6),
+    ("rmul", 1, 0, 2),
+    ("radd", 0, 1),
+    ("rscale", 1, 1, 3),
+    ("kmul", 0, 7),
+    ("rscale", 1, 1, 0),
+    ("kturn", 1, 3),
+    ("rmul", 1, 0, 0),
+    ("kcp", 1, 3),
+    ("kmul", 0, 6),
+    ("krow", 0, 7),
+    ("rscale", 1, 0, 2),
+    ("rmul", 1, 1, 2),
+    ("krow", 0, 6),
+    ("rscale", 1, 0, 0),
+    ("rmul", 1, 0, 1),
+    ("kq", 1, 3),
+    ("rmul", 1, 0, 3),
+    ("rscale", 1, 1, 2),
+    ("row", "x", 4),
+    ("kturn", 0, 3),
+    ("rscale", 1, 0, 1),
+    ("rscale", 1, 0, 3),
+    ("rmul", 1, 1, 1),
+    ("rq", "r", 0, 1),
+    ("kcp", 0, 3),
+    ("turn", "x", 4),
+    ("row", "x", 7),
+    ("rscale", 1, 1, 1),
+    ("zmul", 0, 3),
+    ("lcp", "x", 4),
+    ("radd", 1, 0),
+    ("zmul", 0, 1),
+    ("lq", "x", 2),
+    ("zmul", 0, 0),
+    ("radd", 1, 1),
+    ("zmul", 0, 4),
+    ("zadd", 0, 1),
+    ("kq", 0, 3),
+    ("turn", "x", 7),
+    ("rq", "r", 1, 0),
+    ("zmul", 0, 2),
+    ("zadd", 0, 4),
+    ("lcp", "x", 7),
+    ("zadd", 0, 0),
+    ("lq", "x", 3),
+    ("zact", 0, 0),
+    ("zmul", 0, 5),
+    ("zadd", 0, 2),
+    ("zadd", 0, 3),
+    ("rq", "r", 1, 1),
+    ("zmul", 0, 7),
+    ("zact", 0, 1),
+    ("zadd", 0, 5),
+    ("zbias", 0, 0),
+    ("zmul", 1, 1),
+    ("zadd", 0, 7),
+    ("zact", 0, 2),
+    ("zout", 0, 0),
+    ("zmul", 1, 5),
+    ("zadd", 1, 1),
+    ("zbias", 0, 1),
+    ("zmul", 0, 6),
+    ("zbias", 0, 2),
+    ("zmul", 1, 4),
+    ("zadd", 0, 6),
+    ("zout", 0, 1),
+    ("zact", 0, 3),
+    ("zmul", 1, 6),
+    ("zadd", 1, 4),
+    ("zout", 0, 2),
+    ("zmul", 1, 7),
+    ("zbias", 0, 3),
+    ("zmul", 1, 3),
+    ("zadd", 1, 5),
+    ("zadd", 1, 7),
+    ("zact", 1, 2),
+    ("zadd", 1, 6),
+    ("zmul", 1, 2),
+    ("zout", 0, 3),
+    ("zadd", 1, 3),
+    ("zact", 1, 3),
+    ("zmul", 1, 0),
+    ("zadd", 1, 2),
+    ("zbias", 1, 2),
+    ("zadd", 1, 0),
+    ("zact", 1, 1),
+    ("zbias", 1, 3),
+    ("zout", 1, 2),
+    ("zact", 1, 0),
+    ("zout", 1, 3),
+    ("zbias", 1, 1),
+    ("zbias", 1, 0),
+    ("zout", 1, 1),
+    ("zout", 1, 0),
+]
+SWAP = {("vcopy", "p0"), ("vcopy", "x1"), ("vcopy", "x0"), ("shalf", 0, 1, 1), ("shalf", 1, 0, 1), ("shalf", 1, 0, 0), ("shalf", 1, 0, 2), ("lay", "q0", 1, 1), ("lay", "p1", 1, 1), ("lay", "q1", 1, 1)}
 FLOPS = 4 * 2 * N * D * D
 
 
@@ -30,9 +341,17 @@ def tile_skewexptaylorrecurrentstep_w4_kernel(tc, h, x_bytes, x_scale, a, t_word
         keep = ctx.enter_context(tc.tile_pool(name="keep", bufs=1))
         work = ctx.enter_context(tc.tile_pool(name="work", bufs=2))
         roll = ctx.enter_context(tc.tile_pool(name="roll", bufs=3))
-        psum_s = ctx.enter_context(tc.psum_pool(name="psum_s", bufs=3))
-        psum_t = ctx.enter_context(tc.psum_pool(name="psum_t", bufs=2))
-        psum_a = ctx.enter_context(tc.psum_pool(name="psum_a", bufs=3))
+        psum = ctx.enter_context(tc.psum_pool(name="psum", bufs=8))
+
+
+        ident = keep.tile([P, P], BF16, name="ident")
+        make_identity(nc, ident[:])
+        identf = keep.tile([P, P], F32, name="identf")
+        make_identity(nc, identf[:])
+        negid = keep.tile([P, P], BF16, name="negid")
+        nc.vector.tensor_scalar(out=negid[:], in0=ident[:], scalar1=-1.0, scalar2=None, op0=ALU.mult)
+        ts = keep.tile([P, G, D], U8, name="ts", align_bytes=64)
+        nc.gpsimd.memset(ts[:].rearrange("p g n -> p (g n)").bitcast(I32), 0)
 
         gq = keep.tile([P, 6, T], BF16, name="gq")
         nc.scalar.dma_start(out=gq[:], in_=q.rearrange("i k -> (i k)").rearrange("(a p t) -> p a t", p=P, t=T))
@@ -44,9 +363,9 @@ def tile_skewexptaylorrecurrentstep_w4_kernel(tc, h, x_bytes, x_scale, a, t_word
         hrow = keep.tile([P, J, D], BF16, name="hrow")
 
         def load_a(c, g):
-            t1 = roll.tile([P, T, H], BF16, name="ak", tag="ak")
+            t1 = roll.tile([P, T, H], BF16, name="ak", tag="ak", bufs=4)
             nc.sync.dma_start(out=t1[:], in_=a[g * H:(g + 1) * H, c * H:(c + 1) * H].rearrange("(p t) n -> p t n", t=T))
-            t2 = roll.tile([P, 4, H], BF16, name="ar", tag="ar")
+            t2 = roll.tile([P, 4, H], BF16, name="ar", tag="ar", bufs=4)
             nc.sync.dma_start(out=t2[:], in_=a[c * H:(c + 1) * H, g * H:(g + 1) * H].rearrange("(j p) k -> p j k", p=P))
             ak[c, g] = t1
             ar[c, g] = t2
@@ -54,42 +373,68 @@ def tile_skewexptaylorrecurrentstep_w4_kernel(tc, h, x_bytes, x_scale, a, t_word
         def load_h(j0, j1):
             nc.sync.dma_start(out=hrow[:, j0:j1, :], in_=h[j0 * P:j1 * P, :].rearrange("(j p) k -> p j k", p=P))
 
-        load_a(0, 0)
-        pb0 = keep.tile([P, D], BF16, name="pb0")
-        nc.sync.dma_start(out=pb0[:], in_=p[0, :].partition_broadcast(P))
-        load_h(0, 2)
-        load_h(2, 4)
-        load_a(0, 1)
-        load_h(4, 8)
-        pb2 = keep.tile([P, D], BF16, name="pb2")
-        nc.sync.dma_start(out=pb2[:], in_=p[2, :].partition_broadcast(P))
-        load_a(1, 0)
-        load_a(1, 1)
-        xs = keep.tile([P, D], F32, name="xs")
-        nc.sync.dma_start(out=xs[:], in_=x_scale.rearrange("o k -> (o k)").partition_broadcast(P))
         xbs = []
-        for jp in range(4):
-            xb = roll.tile([P, 2, D], U8, name="xb", tag="xb", bufs=2)
+
+        def load_x(jp):
+            xb = roll.tile([P, 2, D], U8, name="xb", tag="xb", bufs=4)
             nc.sync.dma_start(out=xb[:], in_=x_bytes[2 * jp * P:(2 * jp + 2) * P, :].rearrange("(j p) k -> p j k", p=P))
             xbs.append(xb)
+
+        pcol = keep.tile([P, 8], BF16, name="pcol")
+        nc.scalar.dma_start(out=pcol[:], in_=p[0, :].rearrange("(m p) -> p m", p=P))
+        xcol = keep.tile([P, 8], F32, name="xcol")
+        nc.scalar.dma_start(out=xcol[:], in_=x_scale.rearrange("o k -> (o k)").rearrange("(m p) -> p m", p=P))
+        load_h(0, 1)
+        load_a(0, 0)
+        load_h(1, 2)
+        load_h(2, 4)
+        load_x(0)
+        load_a(0, 1)
+        load_x(1)
+        load_a(1, 0)
+        load_h(4, 6)
+        load_a(1, 1)
+        load_x(2)
+        load_h(6, 8)
+        load_x(3)
+        pb2 = keep.tile([P, D], BF16, name="pb2")
+        nc.sync.dma_start(out=pb2[:], in_=p[2, :].partition_broadcast(P))
+        bb = keep.tile([P, D], BF16, name="bb")
+        nc.sync.dma_start(out=bb[:], in_=b.partition_broadcast(P))
         tw = keep.tile([P, G, 2 * D], U8, name="tw", align_bytes=64)
         nc.sync.dma_start(out=tw[:], in_=t_words.rearrange("g p n -> p g n"))
-        ts = keep.tile([P, G, D], U8, name="ts", align_bytes=64)
-        nc.gpsimd.memset(ts[:].rearrange("p g n -> p (g n)").bitcast(I32), 0)
         for quad in range(4):
             nc.sync.dma_start(
                 out=ts[32 * quad:32 * quad + 4, :, :].bitcast(I32),
                 in_=t_scales[:, 4 * quad:4 * quad + 4, :].rearrange("g r n -> r g n").bitcast(I32),
             )
-        bb = keep.tile([P, D], BF16, name="bb")
-        nc.sync.dma_start(out=bb[:], in_=b.partition_broadcast(P))
 
-        ident = keep.tile([P, P], BF16, name="ident")
-        make_identity(nc, ident[:])
-        identf = keep.tile([P, P], F32, name="identf")
-        make_identity(nc, identf[:])
-        negid = keep.tile([P, P], BF16, name="negid")
-        nc.vector.tensor_scalar(out=negid[:], in0=ident[:], scalar1=-1.0, scalar2=None, op0=ALU.mult)
+        def spread_mul(nm):
+            if nm[0] == "x":
+                bank = psum.tile([P, 4, P], F32, name="bank", tag="bank")
+                for m in range(4):
+                    col = 4 * int(nm[1]) + m
+                    nc.tensor.transpose(bank[:, m, :], xcol[:, col:col + 1].to_broadcast([P, P]), identf[:])
+            else:
+                bank = psum.tile([P, 8, P], BF16, name="bank", tag="bank")
+                for m in range(8):
+                    nc.tensor.transpose(bank[:, m, :], pcol[:, m:m + 1].to_broadcast([P, P]), ident[:])
+            live["vb", nm] = bank
+
+        def spread_copy(nm, on_scalar):
+            bank = live["vb", nm]
+            if nm[0] == "x":
+                o = xs[:, int(nm[1]) * H:(int(nm[1]) + 1) * H]
+            else:
+                o = pb0[:]
+            i = bank[:].rearrange("p m n -> p (m n)")
+            if on_scalar:
+                nc.scalar.copy(out=o, in_=i)
+            else:
+                nc.vector.tensor_copy(out=o, in_=i)
+
+        xs = keep.tile([P, D], F32, name="xs")
+        pb0 = keep.tile([P, D], BF16, name="pb0")
         fq = keep.tile([P, 6, T], F32, name="fq")
         nc.vector.tensor_copy(out=fq[:], in_=gq[:])
         fp = keep.tile([P, G, T], F32, name="fp")
@@ -99,88 +444,152 @@ def tile_skewexptaylorrecurrentstep_w4_kernel(tc, h, x_bytes, x_scale, a, t_word
         fq2s = keep.tile([P, G, T], F32, name="fq2s")
         nc.vector.tensor_scalar(out=fq2s[:], in0=gq[:, 4:6, :], scalar1=1.0 / 6.0, scalar2=None, op0=ALU.mult)
 
-        def operand(name):
+        def right_tiles(name):
             c = keep.tile([P, G, D], U32, name=name + "_c", align_bytes=64)
             s = keep.tile([P, G, D], U8, name=name + "_s", align_bytes=64)
             return c, s
 
-        def left(name):
+        def left_tiles(name):
             c = keep.tile([P, J, G, P], U32, name=name + "_c", align_bytes=64)
             s = keep.tile([P, J, G, P], U8, name=name + "_s", align_bytes=64)
             return c, s
 
-        q0s, q1s, p1s, q2r = operand("q0s"), operand("q1s"), operand("p1s"), operand("q2r")
-        hp, xp = left("hp"), left("xp")
+        ops = {}
+        for nm in ("q0", "q1", "p1", "r"):
+            ops[nm] = right_tiles(nm)
+        lefts = {"h": left_tiles("h"), "x": left_tiles("x")}
         kp_c = keep.tile([P, G, J, P], U32, name="kp_c", align_bytes=64)
         kp_s = keep.tile([P, G, J, P], U8, name="kp_s", align_bytes=64)
-        sq = keep.tile([P, G, 2, T, H], F32, name="sq")
+        live = {}
 
-        def turn(row, dst, jj, il):
-            words = row.bitcast(F32)
-            bank = psum_t.tile([P, 4, P], F32, name="bank")
+        def left_row(nm, j):
+            row = work.tile([P, D], BF16, name="lrow", tag="lrow", bufs=3, align_bytes=64)
+            live["lrow", nm, j] = row
+            if nm == "h":
+                nc.vector.tensor_tensor(out=row[:], in0=hrow[:, j, :], in1=pb0[:], op=ALU.mult)
+            else:
+                nc.vector.tensor_tensor(out=row[:], in0=xbs[j // 2][:, j % 2, :].bitcast(F8), in1=xs[:], op=ALU.mult)
+
+        def left_turn(nm, j):
+            words = live["lrow", nm, j][:].bitcast(F32)
+            bank = psum.tile([P, 4, P], F32, name="bank", tag="bank")
             for g in range(G):
                 for u in range(2):
                     nc.tensor.transpose(bank[:, 2 * g + u, :], words[:, 256 * g + u:256 * (g + 1):2], identf[:])
+            live["tb", nm, j] = bank
+
+        def left_copy(nm, j):
+            if ("lil", nm, j // 2) not in live:
+                il = work.tile([P, 2, G, P, T], BF16, name="lil", tag="lil", bufs=2, align_bytes=64)
+                live["lil", nm, j // 2] = il
+            il = live["lil", nm, j // 2]
+            bank = live["tb", nm, j]
             nc.scalar.copy(
-                out=il[:, jj, :, :, :].rearrange("p g n t -> p g (n t)").bitcast(F32).rearrange("p g (n u) -> p g n u", u=2),
+                out=il[:, j % 2, :, :, :].rearrange("p g n t -> p g (n t)").bitcast(F32).rearrange("p g (n u) -> p g n u", u=2),
                 in_=bank[:].rearrange("p (g u) n -> p g n u", u=2),
             )
 
-        def do_left(jp, dst, make_row):
-            il = work.tile([P, 2, G, P, T], BF16, name="lil", align_bytes=64)
-            for jj in range(2):
-                row = work.tile([P, D], BF16, name="lrow", align_bytes=64)
-                make_row(2 * jp + jj, row)
-                turn(row[:], dst, jj, il)
+        def left_quant(nm, jp):
+            c, s = lefts[nm]
             nc.vector.quantize_mx(
-                out=dst[0][:, 2 * jp:2 * jp + 2, :, :].rearrange("p j g n -> p (j g n)").bitcast(E4X4),
-                scales=dst[1][:, 2 * jp:2 * jp + 2, :, :].rearrange("p j g n -> p (j g n)"),
-                in_=il[:].rearrange("p j g n t -> p (j g n t)"),
+                out=c[:, 2 * jp:2 * jp + 2, :, :].rearrange("p j g n -> p (j g n)").bitcast(E4X4),
+                scales=s[:, 2 * jp:2 * jp + 2, :, :].rearrange("p j g n -> p (j g n)"),
+                in_=live["lil", nm, jp][:].rearrange("p j g n t -> p (j g n t)"),
             )
 
-        def h_row(j, row):
-            nc.vector.tensor_tensor(out=row[:], in0=hrow[:, j, :], in1=pb0[:], op=ALU.mult)
+        bgains = {"p1": fp[:], "q0": gq[:, 0:2, :], "q1": gq[:, 2:4, :]}
+        gains = {"p1": fp, "q0": fq[:, 0:2, :], "q1": fq[:, 2:4, :]}
 
-        def x_row(j, row):
-            nc.vector.tensor_tensor(out=row[:], in0=xbs[j // 2][:, j % 2, :].bitcast(F8), in1=xs[:], op=ALU.mult)
+        def forms(c, again):
+            return ("q0", "p1", "q1") if c == 0 else ("q1",) if again else ("q0", "p1")
 
-        def quant_right(op, g, c, il):
-            nc.vector.quantize_mx(
-                out=op[0][:, g, c * H:(c + 1) * H].bitcast(E4X4),
-                scales=op[1][:, g, c * H:(c + 1) * H],
-                in_=il[:].rearrange("p n t -> p (n t)"),
-            )
+        def s_mul(c, g, t, again=False):
+            bank = psum.tile([P, H], F32, name="bank", tag="bank")
+            nc.tensor.matmul(bank[:], lhsT=ident[:], rhs=ak[c, g][:, t, :], start=True, stop=False)
+            for jj in range(4):
+                nc.tensor.matmul(bank[:, jj * P:(jj + 1) * P], lhsT=ar[c, g][:, jj, t::T], rhs=negid[:], start=False, stop=(jj == 3))
+            live["sb", c, g, t, again] = bank
 
-        def s_group(c, g):
-            pl = {}
-            for nm in ("p1", "q0", "q1"):
-                pl[nm] = work.tile([P, T, H], BF16, name="pl", tag="pl", bufs=4)
-            for t in range(T):
-                bank = psum_s.tile([P, H], F32, name="sbank")
-                nc.tensor.matmul(bank[:], lhsT=ident[:], rhs=ak[c, g][:, t, :], start=True, stop=False)
-                for jj in range(4):
-                    nc.tensor.matmul(bank[:, jj * P:(jj + 1) * P], lhsT=ar[c, g][:, jj, t::T], rhs=negid[:], start=False, stop=(jj == 3))
-                nc.scalar.activation(out=pl["p1"][:, t, :], in_=bank[:], func=ACT.Copy, scale=fp[:, g, t:t + 1])
-                nc.scalar.activation(out=pl["q1"][:, t, :], in_=bank[:], func=ACT.Copy, scale=fq[:, 2 + g, t:t + 1])
-                nc.scalar.activation(out=pl["q0"][:, t, :], in_=bank[:], func=ACT.Copy, scale=fq[:, g, t:t + 1])
-                nc.scalar.activation(out=sq[:, g, c, t, :], in_=bank[:], func=ACT.Copy, scale=fq2h[:, g, t:t + 1])
-            ils = {}
-            for nm in ("p1", "q0", "q1"):
-                il = work.tile([P, H, T], BF16, name="il", tag="il", bufs=3, align_bytes=64)
+        def s_scale(c, g, t, again=False):
+            bank = live["sb", c, g, t, again]
+            for nm in forms(c, again):
+                if ("pl", nm, c, g) not in live:
+                    pl = work.tile([P, T, H], BF16, name="pl", tag="pl", bufs=5)
+                    live["pl", nm, c, g] = pl
+            for nm in forms(c, again):
+                o = live["pl", nm, c, g][:, t, :]
+                i = bank[:]
                 if nm == "p1":
-                    nc.vector.tensor_copy(
-                        out=il[:].rearrange("p (tt m) t -> p tt m t", tt=T),
-                        in_=pl[nm][:].rearrange("p t (m tt) -> p tt m t", tt=T),
-                    )
-                else:
-                    nc.vector.tensor_copy(
-                        out=il[:].rearrange("p (c i) t -> p c t i", i=4),
-                        in_=pl[nm][:].rearrange("p t (c i) -> p c t i", i=4),
-                    )
-                ils[nm] = il
-            quant_right(p1s, g, c, ils["p1"])
-            quant_right(q0s, g, c, ils["q0"])
-            quant_right(q1s, g, c, ils["q1"])
+                    o = o.rearrange("p (tt m) -> p tt m", tt=T)
+                    i = i.rearrange("p (m tt) -> p tt m", tt=T)
+                nc.scalar.activation(out=o, in_=i, func=ACT.Copy, scale=gains[nm][:, g, t:t + 1])
+
+        def s_half(c, g, t, on_vector):
+            bank = live["sb", c, g, t, c == 1]
+            if ("sq", c, g) not in live:
+                sq = work.tile([P, T, H], F32, name="sq", tag="sq", bufs=3)
+                live["sq", c, g] = sq
+            sq = live["sq", c, g]
+            if on_vector:
+                nc.vector.tensor_scalar(out=sq[:, t, :], in0=bank[:], scalar1=fq2h[:, g, t:t + 1], scalar2=None, op0=ALU.mult)
+            else:
+                nc.scalar.activation(out=sq[:, t, :], in_=bank[:], func=ACT.Copy, scale=fq2h[:, g, t:t + 1])
+
+        def w_mul(c, g, jj):
+            bank = psum.tile([P, T, P], F32, name="bank", tag="bank")
+            live["wb", c, g, jj] = bank
+            nc.tensor.matmul(bank[:], lhsT=ident[:], rhs=ak[c, g][:, :, jj * P:(jj + 1) * P], start=True, stop=False)
+            for t in range(T):
+                nc.tensor.matmul(bank[:, t, :], lhsT=ar[c, g][:, jj, t::T], rhs=negid[:], start=False, stop=(t == T - 1))
+
+        def w_gain(nm, c, g, jj):
+            bank = live["wb", c, g, jj]
+            if ("il", nm, c, g) not in live:
+                il = work.tile([P, H, T], BF16, name="il", tag="il", bufs=3, align_bytes=64)
+                live["il", nm, c, g] = il
+            il = live["il", nm, c, g]
+            gain = bgains[nm][:, g, :]
+            if nm == "p1":
+                nc.vector.tensor_tensor(
+                    out=il[:].rearrange("p (tt m) t -> p tt m t", tt=T)[:, :, 32 * jj:32 * (jj + 1), :],
+                    in0=bank[:].rearrange("p t (m tt) -> p tt m t", tt=T),
+                    in1=gain.unsqueeze(1).unsqueeze(1).to_broadcast([P, T, 32, T]),
+                    op=ALU.mult,
+                )
+            else:
+                nc.vector.tensor_tensor(
+                    out=il[:, jj * P:(jj + 1) * P, :],
+                    in0=bank[:].rearrange("p t n -> p n t"),
+                    in1=gain.unsqueeze(1).to_broadcast([P, P, T]),
+                    op=ALU.mult,
+                )
+
+        def w_half(c, g, jj):
+            bank = live["wb", c, g, jj]
+            if ("sq", c, g) not in live:
+                sq = work.tile([P, T, H], F32, name="sq", tag="sq", bufs=3)
+                live["sq", c, g] = sq
+            for t in range(T):
+                nc.scalar.activation(out=live["sq", c, g][:, t, jj * P:(jj + 1) * P], in_=bank[:, t, :], func=ACT.Copy, scale=fq2h[:, g, t:t + 1])
+
+        def lay(nm, c, g, on_scalar=False):
+            il = work.tile([P, H, T], BF16, name="il", tag="il", bufs=3, align_bytes=64)
+            live["il", nm, c, g] = il
+            pl = live["pl", nm, c, g]
+            o = il[:].rearrange("p (c i) t -> p c t i", i=4)
+            i = pl[:].rearrange("p t (c i) -> p c t i", i=4)
+            if on_scalar:
+                nc.scalar.copy(out=o, in_=i)
+            else:
+                nc.vector.tensor_copy(out=o, in_=i)
+
+        def right_quant(nm, c, g):
+            cc, ss = ops[nm]
+            nc.vector.quantize_mx(
+                out=cc[:, g, c * H:(c + 1) * H].bitcast(E4X4),
+                scales=ss[:, g, c * H:(c + 1) * H],
+                in_=live["il", nm, c, g][:].rearrange("p n t -> p (n t)"),
+            )
 
         def mx(acc, lc, ls, rc, rs, first, last, fp4=False):
             nc.tensor.matmul_mx(
@@ -190,97 +599,165 @@ def tile_skewexptaylorrecurrentstep_w4_kernel(tc, h, x_bytes, x_scale, a, t_word
                 start=first, stop=last,
             )
 
-        def right(op, g, c):
-            return op[0][:, g, c * H:(c + 1) * H], op[1][:, g, c * H:(c + 1) * H]
+        def right(nm, g, c):
+            return ops[nm][0][:, g, c * H:(c + 1) * H], ops[nm][1][:, g, c * H:(c + 1) * H]
 
-        def k_pair(c, jp):
-            il = work.tile([P, 2, P, T], BF16, name="kil", align_bytes=64)
-            bank = psum_t.tile([P, 4, P], F32, name="bank")
+        def k_mul(c, j):
+            acc = psum.tile([P, H], F32, name="bank", tag="bank")
+            for g in range(G):
+                rc, rs = right("q0", g, c)
+                mx(acc[:], lefts["h"][0][:, j, g, :], lefts["h"][1][:, j, g, :], rc, rs, g == 0, g == 1)
+            live["kacc", c, j] = acc
+
+        def k_row(c, j):
+            row = work.tile([P, H], BF16, name="krow", tag="krow", bufs=3, align_bytes=64)
+            live["krow", c, j] = row
+            nc.vector.tensor_tensor(out=row[:], in0=live["kacc", c, j][:], in1=pb2[:, c * H:(c + 1) * H], op=ALU.mult)
+
+        def k_turn(c, jp):
+            bank = psum.tile([P, 4, P], F32, name="bank", tag="bank")
             for jj in range(2):
-                j = 2 * jp + jj
-                acc = psum_a.tile([P, H], F32, name="acc")
-                for g in range(G):
-                    rc, rs = right(q0s, g, c)
-                    mx(acc[:], hp[0][:, j, g, :], hp[1][:, j, g, :], rc, rs, g == 0, g == 1)
-                row = work.tile([P, H], BF16, name="krow", align_bytes=64)
-                nc.vector.tensor_tensor(out=row[:], in0=acc[:], in1=pb2[:, c * H:(c + 1) * H], op=ALU.mult)
-                words = row[:].bitcast(F32)
+                words = live["krow", c, 2 * jp + jj][:].bitcast(F32)
                 for u in range(2):
                     nc.tensor.transpose(bank[:, 2 * jj + u, :], words[:, u::2], identf[:])
+            live["kb", c, jp] = bank
+
+        def k_copy(c, jp):
+            il = work.tile([P, 2, P, T], BF16, name="kil", align_bytes=64)
+            live["kil", c, jp] = il
+            bank = live["kb", c, jp]
             nc.scalar.copy(
                 out=il[:].rearrange("p j n t -> p j (n t)").bitcast(F32).rearrange("p j (n u) -> p j n u", u=2),
                 in_=bank[:].rearrange("p (j u) n -> p j n u", u=2),
             )
+
+        def k_quant(c, jp):
             nc.vector.quantize_mx(
                 out=kp_c[:, c, 2 * jp:2 * jp + 2, :].rearrange("p j n -> p (j n)").bitcast(E4X4),
                 scales=kp_s[:, c, 2 * jp:2 * jp + 2, :].rearrange("p j n -> p (j n)"),
-                in_=il[:].rearrange("p j n t -> p (j n t)"),
+                in_=live["kil", c, jp][:].rearrange("p j n t -> p (j n t)"),
             )
 
-        def r_group(c, gm):
-            rq = work.tile([P, T, H], F32, name="rq")
-            for t in range(T):
-                acc = psum_a.tile([P, H], F32, name="acc")
-                m0 = gm * H + t * P
-                for g in range(G):
-                    rc, rs = right(q1s, g, c)
-                    mx(acc[:], p1s[0][:, g, m0:m0 + P], p1s[1][:, g, m0:m0 + P], rc, rs, g == 0, g == 1)
-                nc.scalar.activation(out=rq[:, t, :], in_=acc[:], func=ACT.Copy, scale=fq2s[:, gm, t:t + 1])
+        def r_part(c, gm, t):
+            acc = psum.tile([P, H], F32, name="bank", tag="bank")
+            m0 = gm * H + t * P
+            for g in range(G):
+                rc, rs = right("q1", g, c)
+                mx(acc[:], ops["p1"][0][:, g, m0:m0 + P], ops["p1"][1][:, g, m0:m0 + P], rc, rs, g == 0, g == 1)
+            live["racc", c, gm, t] = acc
+
+        def r_scale(c, gm, t):
+            acc = live["racc", c, gm, t]
+            if ("rq", c, gm) not in live:
+                rq = work.tile([P, T, H], F32, name="rq")
+                live["rq", c, gm] = rq
+            nc.scalar.activation(out=live["rq", c, gm][:, t, :], in_=acc[:], func=ACT.Copy, scale=fq2s[:, gm, t:t + 1])
+
+        def r_add(c, gm):
             il = work.tile([P, H, T], BF16, name="il", tag="il", bufs=3, align_bytes=64)
+            live["il", "r", c, gm] = il
             nc.vector.tensor_tensor(
-                out=il[:],
-                in0=rq[:].rearrange("p t n -> p n t"),
-                in1=sq[:, gm, c, :, :].rearrange("p t n -> p n t"),
+                out=il[:].rearrange("p (c i) t -> p c t i", i=4),
+                in0=live["rq", c, gm][:].rearrange("p t (c i) -> p c t i", i=4),
+                in1=live["sq", c, gm][:].rearrange("p t (c i) -> p c t i", i=4),
                 op=ALU.add,
             )
-            quant_right(q2r, gm, c, il)
 
-        def z_pair(c, jp):
+        def z_mul(c, j):
             cs = slice(c * H, (c + 1) * H)
-            z = roll.tile([P, 2, H], F32, name="z", tag="ak")
-            for jj in range(2):
-                j = 2 * jp + jj
-                acc = psum_a.tile([P, H], F32, name="acc")
-                for g in range(G):
-                    rc, rs = right(q0s, g, c)
-                    mx(acc[:], hp[0][:, j, g, :], hp[1][:, j, g, :], rc, rs, g == 0, False)
-                for g in range(G):
-                    mx(acc[:], xp[0][:, j, g, :], xp[1][:, j, g, :], tw[:, g, 2 * c * H:2 * (c + 1) * H], ts[:, g, cs], False, False, True)
-                for g in range(G):
-                    rc, rs = right(q2r, g, c)
-                    mx(acc[:], kp_c[:, g, j, :], kp_s[:, g, j, :], rc, rs, False, g == 1)
-                nc.vector.tensor_tensor(out=z[:, jj, :], in0=acc[:], in1=hrow[:, j, cs], op=ALU.add)
-            za = roll.tile([P, 2, H], F32, name="za", tag="ar")
-            nc.scalar.activation(out=za[:], in_=z[:], func=ACT.Abs)
-            sg = roll.tile([P, 2, H], BF16, name="sg")
-            nc.scalar.activation(out=sg[:], in_=z[:], func=ACT.Sign)
-            nc.vector.tensor_tensor(out=za[:], in0=za[:], in1=bb[:, cs].unsqueeze(1).to_broadcast([P, 2, H]), op=ALU.add)
-            nc.vector.scalar_tensor_tensor(out=za[:], in0=za[:], scalar=0.0, in1=sg[:], op0=ALU.max, op1=ALU.mult)
-            nc.sync.dma_start(out=out[2 * jp * P:(2 * jp + 2) * P, cs].rearrange("(j p) d -> p j d", p=P), in_=za[:])
+            acc = psum.tile([P, H], F32, name="bank", tag="bank")
+            live["zacc", c, j] = acc
+            for g in range(G):
+                rc, rs = right("q0", g, c)
+                mx(acc[:], lefts["h"][0][:, j, g, :], lefts["h"][1][:, j, g, :], rc, rs, g == 0, False)
+            for g in range(G):
+                mx(acc[:], lefts["x"][0][:, j, g, :], lefts["x"][1][:, j, g, :], tw[:, g, 2 * c * H:2 * (c + 1) * H], ts[:, g, cs], False, False, True)
+            for g in range(G):
+                rc, rs = right("r", g, c)
+                mx(acc[:], kp_c[:, g, j, :], kp_s[:, g, j, :], rc, rs, False, g == 1)
 
-        s_group(0, 0)
-        do_left(0, hp, h_row)
-        do_left(1, hp, h_row)
-        s_group(0, 1)
-        do_left(2, hp, h_row)
-        do_left(3, hp, h_row)
-        s_group(1, 0)
-        for jp in range(4):
-            k_pair(0, jp)
-        s_group(1, 1)
-        do_left(0, xp, x_row)
-        do_left(1, xp, x_row)
-        r_group(0, 0)
-        r_group(0, 1)
-        do_left(2, xp, x_row)
-        do_left(3, xp, x_row)
-        for jp in range(4):
-            k_pair(1, jp)
-        r_group(1, 0)
-        z_pair(0, 0)
-        z_pair(0, 1)
-        r_group(1, 1)
-        z_pair(0, 2)
-        z_pair(0, 3)
-        for jp in range(4):
-            z_pair(1, jp)
+        def z_add(c, j):
+            if ("z", c, j // 2) not in live:
+                z = roll.tile([P, 2, H], F32, name="z", tag="ak", bufs=4)
+                live["z", c, j // 2] = z
+            nc.vector.tensor_tensor(out=live["z", c, j // 2][:, j % 2, :], in0=live["zacc", c, j][:], in1=hrow[:, j, c * H:(c + 1) * H], op=ALU.add)
+
+        def z_act(c, jp):
+            z = live["z", c, jp]
+            za = roll.tile([P, 2, H], F32, name="za", tag="ar", bufs=4)
+            live["za", c, jp] = za
+            nc.scalar.activation(out=za[:], in_=z[:], func=ACT.Abs)
+            sg = roll.tile([P, 2, H], BF16, name="sg", tag="xb", bufs=4)
+            live["sg", c, jp] = sg
+            nc.scalar.activation(out=sg[:], in_=z[:], func=ACT.Sign)
+
+        def z_bias(c, jp):
+            za = live["za", c, jp]
+            nc.vector.tensor_tensor(out=za[:], in0=za[:], in1=bb[:, c * H:(c + 1) * H].unsqueeze(1).to_broadcast([P, 2, H]), op=ALU.add)
+
+        def z_out(c, jp):
+            za = live["za", c, jp]
+            nc.vector.scalar_tensor_tensor(out=za[:], in0=za[:], scalar=0.0, in1=live["sg", c, jp][:], op0=ALU.max, op1=ALU.mult)
+            nc.sync.dma_start(out=out[2 * jp * P:(2 * jp + 2) * P, c * H:(c + 1) * H].rearrange("(j p) d -> p j d", p=P), in_=za[:])
+
+        todo = {}
+
+        def step(key, fn, *args):
+            todo[key] = (fn, args)
+
+        for c in range(2):
+            for g in range(G):
+                if (c, g) in WIDE:
+                    for jj in range(4):
+                        step(("wmul", c, g, jj), w_mul, c, g, jj)
+                        for nm in ("q0", "p1", "q1"):
+                            step(("wgain", nm, c, g, jj), w_gain, nm, c, g, jj)
+                        step(("whalf", c, g, jj), w_half, c, g, jj)
+                    for nm in ("q0", "p1", "q1"):
+                        step(("rq", nm, c, g), right_quant, nm, c, g)
+                    continue
+                for t in range(T):
+                    step(("smul", c, g, t), s_mul, c, g, t)
+                    step(("sscale", c, g, t), s_scale, c, g, t)
+                    if c == 1:
+                        step(("smulb", c, g, t), s_mul, c, g, t, True)
+                        step(("sscaleb", c, g, t), s_scale, c, g, t, True)
+                    step(("shalf", c, g, t), s_half, c, g, t, ("shalf", c, g, t) in SWAP)
+                for nm in ("q0", "p1", "q1"):
+                    step(("lay", nm, c, g), lay, nm, c, g, ("lay", nm, c, g) in SWAP)
+                    step(("rq", nm, c, g), right_quant, nm, c, g)
+        for nm in ("p0", "x0", "x1"):
+            step(("smulv", nm), spread_mul, nm)
+            step(("vcopy", nm), spread_copy, nm, ("vcopy", nm) in SWAP)
+        for nm in ("h", "x"):
+            for j in range(J):
+                step(("row", nm, j), left_row, nm, j)
+                step(("turn", nm, j), left_turn, nm, j)
+                step(("lcp", nm, j), left_copy, nm, j)
+            for jp in range(4):
+                step(("lq", nm, jp), left_quant, nm, jp)
+        for c in range(2):
+            for j in range(J):
+                step(("kmul", c, j), k_mul, c, j)
+                step(("krow", c, j), k_row, c, j)
+            for jp in range(4):
+                step(("kturn", c, jp), k_turn, c, jp)
+                step(("kcp", c, jp), k_copy, c, jp)
+                step(("kq", c, jp), k_quant, c, jp)
+            for gm in range(G):
+                for t in range(T):
+                    step(("rmul", c, gm, t), r_part, c, gm, t)
+                    step(("rscale", c, gm, t), r_scale, c, gm, t)
+                step(("radd", c, gm), r_add, c, gm)
+                step(("rq", "r", c, gm), right_quant, "r", c, gm)
+            for j in range(J):
+                step(("zmul", c, j), z_mul, c, j)
+                step(("zadd", c, j), z_add, c, j)
+            for jp in range(4):
+                step(("zact", c, jp), z_act, c, jp)
+                step(("zbias", c, jp), z_bias, c, jp)
+                step(("zout", c, jp), z_out, c, jp)
+        with tc.manual_schedule():
+            for step_no in ORDER:
+                fn, args = todo[step_no]
+                fn(*args)

from contextlib import ExitStack

import concourse.mybir as mybir
from concourse.masks import make_identity

F32 = mybir.dt.float32
BF16 = mybir.dt.bfloat16
U32 = mybir.dt.uint32
I32 = mybir.dt.int32
U8 = mybir.dt.uint8
F8 = mybir.dt.float8_e4m3fn
E4X4 = mybir.dt.float8_e4m3fn_x4
E2X4 = mybir.dt.float4_e2m1fn_x4
ALU = mybir.AluOpType
ACT = mybir.ActivationFunctionType

P = 128
N = 1024
D = 1024
J = N // P
G = 2
T = 4
H = 512
WIDE = ((0, 0),)
ORDER = [
    ("smulv", "p0"),
    ("smulv", "x1"),
    ("vcopy", "p0"),
    ("smulv", "x0"),
    ("vcopy", "x1"),
    ("row", "h", 0),
    ("vcopy", "x0"),
    ("wmul", 0, 0, 0),
    ("row", "h", 1),
    ("turn", "h", 0),
    ("whalf", 0, 0, 0),
    ("wgain", "q0", 0, 0, 0),
    ("wmul", 0, 0, 2),
    ("lcp", "h", 0),
    ("wgain", "q1", 0, 0, 0),
    ("wmul", 0, 0, 3),
    ("whalf", 0, 0, 2),
    ("wgain", "q0", 0, 0, 2),
    ("wmul", 0, 0, 1),
    ("wgain", "p1", 0, 0, 0),
    ("whalf", 0, 0, 3),
    ("turn", "h", 1),
    ("wgain", "q1", 0, 0, 1),
    ("whalf", 0, 0, 1),
    ("wgain", "q1", 0, 0, 3),
    ("smul", 0, 1, 2),
    ("lcp", "h", 1),
    ("wgain", "p1", 0, 0, 1),
    ("smul", 0, 1, 0),
    ("lq", "h", 0),
    ("sscale", 0, 1, 2),
    ("smul", 0, 1, 1),
    ("wgain", "q0", 0, 0, 3),
    ("smul", 0, 1, 3),
    ("row", "h", 3),
    ("sscale", 0, 1, 1),
    ("wgain", "p1", 0, 0, 3),
    ("wgain", "q0", 0, 0, 1),
    ("row", "h", 4),
    ("sscale", 0, 1, 0),
    ("rq", "q0", 0, 0),
    ("wgain", "q1", 0, 0, 2),
    ("row", "h", 5),
    ("shalf", 0, 1, 3),
    ("shalf", 0, 1, 1),
    ("sscale", 0, 1, 3),
    ("wgain", "p1", 0, 0, 2),
    ("rq", "q1", 0, 0),
    ("smul", 1, 0, 2),
    ("rq", "p1", 0, 0),
    ("smul", 1, 0, 1),
    ("shalf", 0, 1, 0),
    ("lay", "q0", 0, 1),
    ("smul", 1, 0, 0),
    ("sscale", 1, 0, 2),
    ("smul", 1, 1, 0),
    ("sscale", 1, 0, 0),
    ("lay", "q1", 0, 1),
    ("shalf", 0, 1, 2),
    ("rq", "q0", 0, 1),
    ("sscale", 1, 0, 1),
    ("lay", "p1", 0, 1),
    ("turn", "h", 3),
    ("kmul", 0, 1),
    ("sscale", 1, 1, 0),
    ("smul", 1, 1, 1),
    ("row", "h", 2),
    ("kmul", 0, 0),
    ("krow", 0, 1),
    ("lcp", "h", 3),
    ("smulb", 1, 0, 1),
    ("rq", "q1", 0, 1),
    ("sscale", 1, 1, 1),
    ("turn", "h", 4),
    ("krow", 0, 0),
    ("smul", 1, 0, 3),
    ("sscaleb", 1, 0, 1),
    ("rq", "p1", 0, 1),
    ("kturn", 0, 0),
    ("lcp", "h", 4),
    ("row", "x", 3),
    ("sscale", 1, 0, 3),
    ("rmul", 0, 0, 1),
    ("shalf", 1, 0, 1),
    ("rmul", 0, 0, 0),
    ("rscale", 0, 0, 1),
    ("smulb", 1, 0, 0),
    ("lay", "q0", 1, 0),
    ("rscale", 0, 0, 0),
    ("turn", "h", 2),
    ("kcp", 0, 0),
    ("rmul", 0, 0, 3),
    ("shalf", 1, 0, 0),
    ("sscaleb", 1, 0, 0),
    ("rmul", 0, 0, 2),
    ("kq", 0, 0),
    ("rscale", 0, 0, 3),
    ("turn", "h", 5),
    ("rq", "q0", 1, 0),
    ("rscale", 0, 0, 2),
    ("smul", 1, 1, 2),
    ("lay", "p1", 1, 0),
    ("lcp", "h", 2),
    ("smulb", 1, 0, 3),
    ("lcp", "h", 5),
    ("turn", "x", 3),
    ("sscaleb", 1, 0, 3),
    ("row", "h", 7),
    ("smulb", 1, 1, 2),
    ("sscale", 1, 1, 2),
    ("row", "x", 2),
    ("smulb", 1, 1, 1),
    ("smulb", 1, 1, 0),
    ("sscaleb", 1, 1, 2),
    ("radd", 0, 0),
    ("turn", "x", 2),
    ("sscaleb", 1, 1, 1),
    ("smulb", 1, 0, 2),
    ("sscaleb", 1, 1, 0),
    ("smul", 1, 1, 3),
    ("shalf", 1, 0, 3),
    ("sscaleb", 1, 0, 2),
    ("row", "x", 1),
    ("smulb", 1, 1, 3),
    ("shalf", 1, 1, 1),
    ("sscaleb", 1, 1, 3),
    ("lay", "q1", 1, 0),
    ("shalf", 1, 1, 3),
    ("sscale", 1, 1, 3),
    ("lq", "h", 1),
    ("rq", "q1", 1, 0),
    ("lcp", "x", 2),
    ("shalf", 1, 0, 2),
    ("shalf", 1, 1, 0),
    ("rq", "p1", 1, 0),
    ("shalf", 1, 1, 2),
    ("lq", "h", 2),
    ("lcp", "x", 3),
    ("rq", "r", 0, 0),
    ("lay", "q0", 1, 1),
    ("kmul", 0, 3),
    ("lq", "x", 1),
    ("kmul", 0, 2),
    ("krow", 0, 3),
    ("kmul", 0, 4),
    ("krow", 0, 2),
    ("kmul", 0, 5),
    ("krow", 0, 4),
    ("turn", "x", 1),
    ("lay", "p1", 1, 1),
    ("rq", "q0", 1, 1),
    ("kturn", 0, 1),
    ("turn", "h", 7),
    ("krow", 0, 5),
    ("kmul", 1, 1),
    ("row", "h", 6),
    ("kmul", 1, 0),
    ("kcp", 0, 1),
    ("krow", 1, 1),
    ("kturn", 0, 2),
    ("lcp", "x", 1),
    ("rq", "p1", 1, 1),
    ("kmul", 1, 2),
    ("lcp", "h", 7),
    ("krow", 1, 0),
    ("rmul", 0, 1, 0),
    ("kcp", 0, 2),
    ("kq", 0, 1),
    ("rmul", 0, 1, 2),
    ("krow", 1, 2),
    ("lay", "q1", 1, 1),
    ("kmul", 1, 3),
    ("kq", 0, 2),
    ("row", "x", 0),
    ("kturn", 1, 0),
    ("kmul", 1, 5),
    ("krow", 1, 3),
    ("rmul", 0, 1, 1),
    ("rscale", 0, 1, 0),
    ("krow", 1, 5),
    ("kmul", 1, 4),
    ("rscale", 0, 1, 2),
    ("row", "x", 5),
    ("kturn", 1, 1),
    ("kcp", 1, 0),
    ("turn", "h", 6),
    ("rscale", 0, 1, 1),
    ("krow", 1, 4),
    ("rmul", 0, 1, 3),
    ("kcp", 1, 1),
    ("kq", 1, 0),
    ("kturn", 1, 2),
    ("row", "x", 6),
    ("lcp", "h", 6),
    ("turn", "x", 5),
    ("rscale", 0, 1, 3),
    ("turn", "x", 0),
    ("kq", 1, 1),
    ("kcp", 1, 2),
    ("lq", "h", 3),
    ("turn", "x", 6),
    ("lcp", "x", 0),
    ("kq", 1, 2),
    ("kmul", 1, 6),
    ("rq", "q1", 1, 1),
    ("kmul", 1, 7),
    ("lq", "x", 0),
    ("rmul", 1, 1, 0),
    ("krow", 1, 6),
    ("lcp", "x", 5),
    ("rmul", 1, 1, 3),
    ("krow", 1, 7),
    ("lcp", "x", 6),
    ("rmul", 1, 0, 2),
    ("radd", 0, 1),
    ("rscale", 1, 1, 3),
    ("kmul", 0, 7),
    ("rscale", 1, 1, 0),
    ("kturn", 1, 3),
    ("rmul", 1, 0, 0),
    ("kcp", 1, 3),
    ("kmul", 0, 6),
    ("krow", 0, 7),
    ("rscale", 1, 0, 2),
    ("rmul", 1, 1, 2),
    ("krow", 0, 6),
    ("rscale", 1, 0, 0),
    ("rmul", 1, 0, 1),
    ("kq", 1, 3),
    ("rmul", 1, 0, 3),
    ("rscale", 1, 1, 2),
    ("row", "x", 4),
    ("kturn", 0, 3),
    ("rscale", 1, 0, 1),
    ("rscale", 1, 0, 3),
    ("rmul", 1, 1, 1),
    ("rq", "r", 0, 1),
    ("kcp", 0, 3),
    ("turn", "x", 4),
    ("row", "x", 7),
    ("rscale", 1, 1, 1),
    ("zmul", 0, 3),
    ("lcp", "x", 4),
    ("radd", 1, 0),
    ("zmul", 0, 1),
    ("lq", "x", 2),
    ("zmul", 0, 0),
    ("radd", 1, 1),
    ("zmul", 0, 4),
    ("zadd", 0, 1),
    ("kq", 0, 3),
    ("turn", "x", 7),
    ("rq", "r", 1, 0),
    ("zmul", 0, 2),
    ("zadd", 0, 4),
    ("lcp", "x", 7),
    ("zadd", 0, 0),
    ("lq", "x", 3),
    ("zact", 0, 0),
    ("zmul", 0, 5),
    ("zadd", 0, 2),
    ("zadd", 0, 3),
    ("rq", "r", 1, 1),
    ("zmul", 0, 7),
    ("zact", 0, 1),
    ("zadd", 0, 5),
    ("zbias", 0, 0),
    ("zmul", 1, 1),
    ("zadd", 0, 7),
    ("zact", 0, 2),
    ("zout", 0, 0),
    ("zmul", 1, 5),
    ("zadd", 1, 1),
    ("zbias", 0, 1),
    ("zmul", 0, 6),
    ("zbias", 0, 2),
    ("zmul", 1, 4),
    ("zadd", 0, 6),
    ("zout", 0, 1),
    ("zact", 0, 3),
    ("zmul", 1, 6),
    ("zadd", 1, 4),
    ("zout", 0, 2),
    ("zmul", 1, 7),
    ("zbias", 0, 3),
    ("zmul", 1, 3),
    ("zadd", 1, 5),
    ("zadd", 1, 7),
    ("zact", 1, 2),
    ("zadd", 1, 6),
    ("zmul", 1, 2),
    ("zout", 0, 3),
    ("zadd", 1, 3),
    ("zact", 1, 3),
    ("zmul", 1, 0),
    ("zadd", 1, 2),
    ("zbias", 1, 2),
    ("zadd", 1, 0),
    ("zact", 1, 1),
    ("zbias", 1, 3),
    ("zout", 1, 2),
    ("zact", 1, 0),
    ("zout", 1, 3),
    ("zbias", 1, 1),
    ("zbias", 1, 0),
    ("zout", 1, 1),
    ("zout", 1, 0),
]
SWAP = {("vcopy", "p0"), ("vcopy", "x1"), ("vcopy", "x0"), ("shalf", 0, 1, 1), ("shalf", 1, 0, 1), ("shalf", 1, 0, 0), ("shalf", 1, 0, 2), ("lay", "q0", 1, 1), ("lay", "p1", 1, 1), ("lay", "q1", 1, 1)}
FLOPS = 4 * 2 * N * D * D


def tile_skewexptaylorrecurrentstep_w4_kernel(tc, h, x_bytes, x_scale, a, t_words, t_scales, p, q, b, out):
    nc = tc.nc
    with ExitStack() as ctx:
        keep = ctx.enter_context(tc.tile_pool(name="keep", bufs=1))
        work = ctx.enter_context(tc.tile_pool(name="work", bufs=2))
        roll = ctx.enter_context(tc.tile_pool(name="roll", bufs=3))
        psum = ctx.enter_context(tc.psum_pool(name="psum", bufs=8))


        ident = keep.tile([P, P], BF16, name="ident")
        make_identity(nc, ident[:])
        identf = keep.tile([P, P], F32, name="identf")
        make_identity(nc, identf[:])
        negid = keep.tile([P, P], BF16, name="negid")
        nc.vector.tensor_scalar(out=negid[:], in0=ident[:], scalar1=-1.0, scalar2=None, op0=ALU.mult)
        ts = keep.tile([P, G, D], U8, name="ts", align_bytes=64)
        nc.gpsimd.memset(ts[:].rearrange("p g n -> p (g n)").bitcast(I32), 0)

        gq = keep.tile([P, 6, T], BF16, name="gq")
        nc.scalar.dma_start(out=gq[:], in_=q.rearrange("i k -> (i k)").rearrange("(a p t) -> p a t", p=P, t=T))
        gp = keep.tile([P, G, T], BF16, name="gp")
        nc.scalar.dma_start(out=gp[:], in_=p[1, :].rearrange("(g p t) -> p g t", p=P, t=T))

        ak = {}
        ar = {}
        hrow = keep.tile([P, J, D], BF16, name="hrow")

        def load_a(c, g):
            t1 = roll.tile([P, T, H], BF16, name="ak", tag="ak", bufs=4)
            nc.sync.dma_start(out=t1[:], in_=a[g * H:(g + 1) * H, c * H:(c + 1) * H].rearrange("(p t) n -> p t n", t=T))
            t2 = roll.tile([P, 4, H], BF16, name="ar", tag="ar", bufs=4)
            nc.sync.dma_start(out=t2[:], in_=a[c * H:(c + 1) * H, g * H:(g + 1) * H].rearrange("(j p) k -> p j k", p=P))
            ak[c, g] = t1
            ar[c, g] = t2

        def load_h(j0, j1):
            nc.sync.dma_start(out=hrow[:, j0:j1, :], in_=h[j0 * P:j1 * P, :].rearrange("(j p) k -> p j k", p=P))

        xbs = []

        def load_x(jp):
            xb = roll.tile([P, 2, D], U8, name="xb", tag="xb", bufs=4)
            nc.sync.dma_start(out=xb[:], in_=x_bytes[2 * jp * P:(2 * jp + 2) * P, :].rearrange("(j p) k -> p j k", p=P))
            xbs.append(xb)

        pcol = keep.tile([P, 8], BF16, name="pcol")
        nc.scalar.dma_start(out=pcol[:], in_=p[0, :].rearrange("(m p) -> p m", p=P))
        xcol = keep.tile([P, 8], F32, name="xcol")
        nc.scalar.dma_start(out=xcol[:], in_=x_scale.rearrange("o k -> (o k)").rearrange("(m p) -> p m", p=P))
        load_h(0, 1)
        load_a(0, 0)
        load_h(1, 2)
        load_h(2, 4)
        load_x(0)
        load_a(0, 1)
        load_x(1)
        load_a(1, 0)
        load_h(4, 6)
        load_a(1, 1)
        load_x(2)
        load_h(6, 8)
        load_x(3)
        pb2 = keep.tile([P, D], BF16, name="pb2")
        nc.sync.dma_start(out=pb2[:], in_=p[2, :].partition_broadcast(P))
        bb = keep.tile([P, D], BF16, name="bb")
        nc.sync.dma_start(out=bb[:], in_=b.partition_broadcast(P))
        tw = keep.tile([P, G, 2 * D], U8, name="tw", align_bytes=64)
        nc.sync.dma_start(out=tw[:], in_=t_words.rearrange("g p n -> p g n"))
        for quad in range(4):
            nc.sync.dma_start(
                out=ts[32 * quad:32 * quad + 4, :, :].bitcast(I32),
                in_=t_scales[:, 4 * quad:4 * quad + 4, :].rearrange("g r n -> r g n").bitcast(I32),
            )

        def spread_mul(nm):
            if nm[0] == "x":
                bank = psum.tile([P, 4, P], F32, name="bank", tag="bank")
                for m in range(4):
                    col = 4 * int(nm[1]) + m
                    nc.tensor.transpose(bank[:, m, :], xcol[:, col:col + 1].to_broadcast([P, P]), identf[:])
            else:
                bank = psum.tile([P, 8, P], BF16, name="bank", tag="bank")
                for m in range(8):
                    nc.tensor.transpose(bank[:, m, :], pcol[:, m:m + 1].to_broadcast([P, P]), ident[:])
            live["vb", nm] = bank

        def spread_copy(nm, on_scalar):
            bank = live["vb", nm]
            if nm[0] == "x":
                o = xs[:, int(nm[1]) * H:(int(nm[1]) + 1) * H]
            else:
                o = pb0[:]
            i = bank[:].rearrange("p m n -> p (m n)")
            if on_scalar:
                nc.scalar.copy(out=o, in_=i)
            else:
                nc.vector.tensor_copy(out=o, in_=i)

        xs = keep.tile([P, D], F32, name="xs")
        pb0 = keep.tile([P, D], BF16, name="pb0")
        fq = keep.tile([P, 6, T], F32, name="fq")
        nc.vector.tensor_copy(out=fq[:], in_=gq[:])
        fp = keep.tile([P, G, T], F32, name="fp")
        nc.vector.tensor_scalar(out=fp[:], in0=gp[:], scalar1=-1.0, scalar2=None, op0=ALU.mult)
        fq2h = keep.tile([P, G, T], F32, name="fq2h")
        nc.vector.tensor_scalar(out=fq2h[:], in0=gq[:, 4:6, :], scalar1=0.5, scalar2=None, op0=ALU.mult)
        fq2s = keep.tile([P, G, T], F32, name="fq2s")
        nc.vector.tensor_scalar(out=fq2s[:], in0=gq[:, 4:6, :], scalar1=1.0 / 6.0, scalar2=None, op0=ALU.mult)

        def right_tiles(name):
            c = keep.tile([P, G, D], U32, name=name + "_c", align_bytes=64)
            s = keep.tile([P, G, D], U8, name=name + "_s", align_bytes=64)
            return c, s

        def left_tiles(name):
            c = keep.tile([P, J, G, P], U32, name=name + "_c", align_bytes=64)
            s = keep.tile([P, J, G, P], U8, name=name + "_s", align_bytes=64)
            return c, s

        ops = {}
        for nm in ("q0", "q1", "p1", "r"):
            ops[nm] = right_tiles(nm)
        lefts = {"h": left_tiles("h"), "x": left_tiles("x")}
        kp_c = keep.tile([P, G, J, P], U32, name="kp_c", align_bytes=64)
        kp_s = keep.tile([P, G, J, P], U8, name="kp_s", align_bytes=64)
        live = {}

        def left_row(nm, j):
            row = work.tile([P, D], BF16, name="lrow", tag="lrow", bufs=3, align_bytes=64)
            live["lrow", nm, j] = row
            if nm == "h":
                nc.vector.tensor_tensor(out=row[:], in0=hrow[:, j, :], in1=pb0[:], op=ALU.mult)
            else:
                nc.vector.tensor_tensor(out=row[:], in0=xbs[j // 2][:, j % 2, :].bitcast(F8), in1=xs[:], op=ALU.mult)

        def left_turn(nm, j):
            words = live["lrow", nm, j][:].bitcast(F32)
            bank = psum.tile([P, 4, P], F32, name="bank", tag="bank")
            for g in range(G):
                for u in range(2):
                    nc.tensor.transpose(bank[:, 2 * g + u, :], words[:, 256 * g + u:256 * (g + 1):2], identf[:])
            live["tb", nm, j] = bank

        def left_copy(nm, j):
            if ("lil", nm, j // 2) not in live:
                il = work.tile([P, 2, G, P, T], BF16, name="lil", tag="lil", bufs=2, align_bytes=64)
                live["lil", nm, j // 2] = il
            il = live["lil", nm, j // 2]
            bank = live["tb", nm, j]
            nc.scalar.copy(
                out=il[:, j % 2, :, :, :].rearrange("p g n t -> p g (n t)").bitcast(F32).rearrange("p g (n u) -> p g n u", u=2),
                in_=bank[:].rearrange("p (g u) n -> p g n u", u=2),
            )

        def left_quant(nm, jp):
            c, s = lefts[nm]
            nc.vector.quantize_mx(
                out=c[:, 2 * jp:2 * jp + 2, :, :].rearrange("p j g n -> p (j g n)").bitcast(E4X4),
                scales=s[:, 2 * jp:2 * jp + 2, :, :].rearrange("p j g n -> p (j g n)"),
                in_=live["lil", nm, jp][:].rearrange("p j g n t -> p (j g n t)"),
            )

        bgains = {"p1": fp[:], "q0": gq[:, 0:2, :], "q1": gq[:, 2:4, :]}
        gains = {"p1": fp, "q0": fq[:, 0:2, :], "q1": fq[:, 2:4, :]}

        def forms(c, again):
            return ("q0", "p1", "q1") if c == 0 else ("q1",) if again else ("q0", "p1")

        def s_mul(c, g, t, again=False):
            bank = psum.tile([P, H], F32, name="bank", tag="bank")
            nc.tensor.matmul(bank[:], lhsT=ident[:], rhs=ak[c, g][:, t, :], start=True, stop=False)
            for jj in range(4):
                nc.tensor.matmul(bank[:, jj * P:(jj + 1) * P], lhsT=ar[c, g][:, jj, t::T], rhs=negid[:], start=False, stop=(jj == 3))
            live["sb", c, g, t, again] = bank

        def s_scale(c, g, t, again=False):
            bank = live["sb", c, g, t, again]
            for nm in forms(c, again):
                if ("pl", nm, c, g) not in live:
                    pl = work.tile([P, T, H], BF16, name="pl", tag="pl", bufs=5)
                    live["pl", nm, c, g] = pl
            for nm in forms(c, again):
                o = live["pl", nm, c, g][:, t, :]
                i = bank[:]
                if nm == "p1":
                    o = o.rearrange("p (tt m) -> p tt m", tt=T)
                    i = i.rearrange("p (m tt) -> p tt m", tt=T)
                nc.scalar.activation(out=o, in_=i, func=ACT.Copy, scale=gains[nm][:, g, t:t + 1])

        def s_half(c, g, t, on_vector):
            bank = live["sb", c, g, t, c == 1]
            if ("sq", c, g) not in live:
                sq = work.tile([P, T, H], F32, name="sq", tag="sq", bufs=3)
                live["sq", c, g] = sq
            sq = live["sq", c, g]
            if on_vector:
                nc.vector.tensor_scalar(out=sq[:, t, :], in0=bank[:], scalar1=fq2h[:, g, t:t + 1], scalar2=None, op0=ALU.mult)
            else:
                nc.scalar.activation(out=sq[:, t, :], in_=bank[:], func=ACT.Copy, scale=fq2h[:, g, t:t + 1])

        def w_mul(c, g, jj):
            bank = psum.tile([P, T, P], F32, name="bank", tag="bank")
            live["wb", c, g, jj] = bank
            nc.tensor.matmul(bank[:], lhsT=ident[:], rhs=ak[c, g][:, :, jj * P:(jj + 1) * P], start=True, stop=False)
            for t in range(T):
                nc.tensor.matmul(bank[:, t, :], lhsT=ar[c, g][:, jj, t::T], rhs=negid[:], start=False, stop=(t == T - 1))

        def w_gain(nm, c, g, jj):
            bank = live["wb", c, g, jj]
            if ("il", nm, c, g) not in live:
                il = work.tile([P, H, T], BF16, name="il", tag="il", bufs=3, align_bytes=64)
                live["il", nm, c, g] = il
            il = live["il", nm, c, g]
            gain = bgains[nm][:, g, :]
            if nm == "p1":
                nc.vector.tensor_tensor(
                    out=il[:].rearrange("p (tt m) t -> p tt m t", tt=T)[:, :, 32 * jj:32 * (jj + 1), :],
                    in0=bank[:].rearrange("p t (m tt) -> p tt m t", tt=T),
                    in1=gain.unsqueeze(1).unsqueeze(1).to_broadcast([P, T, 32, T]),
                    op=ALU.mult,
                )
            else:
                nc.vector.tensor_tensor(
                    out=il[:, jj * P:(jj + 1) * P, :],
                    in0=bank[:].rearrange("p t n -> p n t"),
                    in1=gain.unsqueeze(1).to_broadcast([P, P, T]),
                    op=ALU.mult,
                )

        def w_half(c, g, jj):
            bank = live["wb", c, g, jj]
            if ("sq", c, g) not in live:
                sq = work.tile([P, T, H], F32, name="sq", tag="sq", bufs=3)
                live["sq", c, g] = sq
            for t in range(T):
                nc.scalar.activation(out=live["sq", c, g][:, t, jj * P:(jj + 1) * P], in_=bank[:, t, :], func=ACT.Copy, scale=fq2h[:, g, t:t + 1])

        def lay(nm, c, g, on_scalar=False):
            il = work.tile([P, H, T], BF16, name="il", tag="il", bufs=3, align_bytes=64)
            live["il", nm, c, g] = il
            pl = live["pl", nm, c, g]
            o = il[:].rearrange("p (c i) t -> p c t i", i=4)
            i = pl[:].rearrange("p t (c i) -> p c t i", i=4)
            if on_scalar:
                nc.scalar.copy(out=o, in_=i)
            else:
                nc.vector.tensor_copy(out=o, in_=i)

        def right_quant(nm, c, g):
            cc, ss = ops[nm]
            nc.vector.quantize_mx(
                out=cc[:, g, c * H:(c + 1) * H].bitcast(E4X4),
                scales=ss[:, g, c * H:(c + 1) * H],
                in_=live["il", nm, c, g][:].rearrange("p n t -> p (n t)"),
            )

        def mx(acc, lc, ls, rc, rs, first, last, fp4=False):
            nc.tensor.matmul_mx(
                out=acc,
                lhsT=lc.bitcast(E4X4), lhsT_scale=ls,
                rhs=rc.bitcast(E2X4 if fp4 else E4X4), rhs_scale=rs,
                start=first, stop=last,
            )

        def right(nm, g, c):
            return ops[nm][0][:, g, c * H:(c + 1) * H], ops[nm][1][:, g, c * H:(c + 1) * H]

        def k_mul(c, j):
            acc = psum.tile([P, H], F32, name="bank", tag="bank")
            for g in range(G):
                rc, rs = right("q0", g, c)
                mx(acc[:], lefts["h"][0][:, j, g, :], lefts["h"][1][:, j, g, :], rc, rs, g == 0, g == 1)
            live["kacc", c, j] = acc

        def k_row(c, j):
            row = work.tile([P, H], BF16, name="krow", tag="krow", bufs=3, align_bytes=64)
            live["krow", c, j] = row
            nc.vector.tensor_tensor(out=row[:], in0=live["kacc", c, j][:], in1=pb2[:, c * H:(c + 1) * H], op=ALU.mult)

        def k_turn(c, jp):
            bank = psum.tile([P, 4, P], F32, name="bank", tag="bank")
            for jj in range(2):
                words = live["krow", c, 2 * jp + jj][:].bitcast(F32)
                for u in range(2):
                    nc.tensor.transpose(bank[:, 2 * jj + u, :], words[:, u::2], identf[:])
            live["kb", c, jp] = bank

        def k_copy(c, jp):
            il = work.tile([P, 2, P, T], BF16, name="kil", align_bytes=64)
            live["kil", c, jp] = il
            bank = live["kb", c, jp]
            nc.scalar.copy(
                out=il[:].rearrange("p j n t -> p j (n t)").bitcast(F32).rearrange("p j (n u) -> p j n u", u=2),
                in_=bank[:].rearrange("p (j u) n -> p j n u", u=2),
            )

        def k_quant(c, jp):
            nc.vector.quantize_mx(
                out=kp_c[:, c, 2 * jp:2 * jp + 2, :].rearrange("p j n -> p (j n)").bitcast(E4X4),
                scales=kp_s[:, c, 2 * jp:2 * jp + 2, :].rearrange("p j n -> p (j n)"),
                in_=live["kil", c, jp][:].rearrange("p j n t -> p (j n t)"),
            )

        def r_part(c, gm, t):
            acc = psum.tile([P, H], F32, name="bank", tag="bank")
            m0 = gm * H + t * P
            for g in range(G):
                rc, rs = right("q1", g, c)
                mx(acc[:], ops["p1"][0][:, g, m0:m0 + P], ops["p1"][1][:, g, m0:m0 + P], rc, rs, g == 0, g == 1)
            live["racc", c, gm, t] = acc

        def r_scale(c, gm, t):
            acc = live["racc", c, gm, t]
            if ("rq", c, gm) not in live:
                rq = work.tile([P, T, H], F32, name="rq")
                live["rq", c, gm] = rq
            nc.scalar.activation(out=live["rq", c, gm][:, t, :], in_=acc[:], func=ACT.Copy, scale=fq2s[:, gm, t:t + 1])

        def r_add(c, gm):
            il = work.tile([P, H, T], BF16, name="il", tag="il", bufs=3, align_bytes=64)
            live["il", "r", c, gm] = il
            nc.vector.tensor_tensor(
                out=il[:].rearrange("p (c i) t -> p c t i", i=4),
                in0=live["rq", c, gm][:].rearrange("p t (c i) -> p c t i", i=4),
                in1=live["sq", c, gm][:].rearrange("p t (c i) -> p c t i", i=4),
                op=ALU.add,
            )

        def z_mul(c, j):
            cs = slice(c * H, (c + 1) * H)
            acc = psum.tile([P, H], F32, name="bank", tag="bank")
            live["zacc", c, j] = acc
            for g in range(G):
                rc, rs = right("q0", g, c)
                mx(acc[:], lefts["h"][0][:, j, g, :], lefts["h"][1][:, j, g, :], rc, rs, g == 0, False)
            for g in range(G):
                mx(acc[:], lefts["x"][0][:, j, g, :], lefts["x"][1][:, j, g, :], tw[:, g, 2 * c * H:2 * (c + 1) * H], ts[:, g, cs], False, False, True)
            for g in range(G):
                rc, rs = right("r", g, c)
                mx(acc[:], kp_c[:, g, j, :], kp_s[:, g, j, :], rc, rs, False, g == 1)

        def z_add(c, j):
            if ("z", c, j // 2) not in live:
                z = roll.tile([P, 2, H], F32, name="z", tag="ak", bufs=4)
                live["z", c, j // 2] = z
            nc.vector.tensor_tensor(out=live["z", c, j // 2][:, j % 2, :], in0=live["zacc", c, j][:], in1=hrow[:, j, c * H:(c + 1) * H], op=ALU.add)

        def z_act(c, jp):
            z = live["z", c, jp]
            za = roll.tile([P, 2, H], F32, name="za", tag="ar", bufs=4)
            live["za", c, jp] = za
            nc.scalar.activation(out=za[:], in_=z[:], func=ACT.Abs)
            sg = roll.tile([P, 2, H], BF16, name="sg", tag="xb", bufs=4)
            live["sg", c, jp] = sg
            nc.scalar.activation(out=sg[:], in_=z[:], func=ACT.Sign)

        def z_bias(c, jp):
            za = live["za", c, jp]
            nc.vector.tensor_tensor(out=za[:], in0=za[:], in1=bb[:, c * H:(c + 1) * H].unsqueeze(1).to_broadcast([P, 2, H]), op=ALU.add)

        def z_out(c, jp):
            za = live["za", c, jp]
            nc.vector.scalar_tensor_tensor(out=za[:], in0=za[:], scalar=0.0, in1=live["sg", c, jp][:], op0=ALU.max, op1=ALU.mult)
            nc.sync.dma_start(out=out[2 * jp * P:(2 * jp + 2) * P, c * H:(c + 1) * H].rearrange("(j p) d -> p j d", p=P), in_=za[:])

        todo = {}

        def step(key, fn, *args):
            todo[key] = (fn, args)

        for c in range(2):
            for g in range(G):
                if (c, g) in WIDE:
                    for jj in range(4):
                        step(("wmul", c, g, jj), w_mul, c, g, jj)
                        for nm in ("q0", "p1", "q1"):
                            step(("wgain", nm, c, g, jj), w_gain, nm, c, g, jj)
                        step(("whalf", c, g, jj), w_half, c, g, jj)
                    for nm in ("q0", "p1", "q1"):
                        step(("rq", nm, c, g), right_quant, nm, c, g)
                    continue
                for t in range(T):
                    step(("smul", c, g, t), s_mul, c, g, t)
                    step(("sscale", c, g, t), s_scale, c, g, t)
                    if c == 1:
                        step(("smulb", c, g, t), s_mul, c, g, t, True)
                        step(("sscaleb", c, g, t), s_scale, c, g, t, True)
                    step(("shalf", c, g, t), s_half, c, g, t, ("shalf", c, g, t) in SWAP)
                for nm in ("q0", "p1", "q1"):
                    step(("lay", nm, c, g), lay, nm, c, g, ("lay", nm, c, g) in SWAP)
                    step(("rq", nm, c, g), right_quant, nm, c, g)
        for nm in ("p0", "x0", "x1"):
            step(("smulv", nm), spread_mul, nm)
            step(("vcopy", nm), spread_copy, nm, ("vcopy", nm) in SWAP)
        for nm in ("h", "x"):
            for j in range(J):
                step(("row", nm, j), left_row, nm, j)
                step(("turn", nm, j), left_turn, nm, j)
                step(("lcp", nm, j), left_copy, nm, j)
            for jp in range(4):
                step(("lq", nm, jp), left_quant, nm, jp)
        for c in range(2):
            for j in range(J):
                step(("kmul", c, j), k_mul, c, j)
                step(("krow", c, j), k_row, c, j)
            for jp in range(4):
                step(("kturn", c, jp), k_turn, c, jp)
                step(("kcp", c, jp), k_copy, c, jp)
                step(("kq", c, jp), k_quant, c, jp)
            for gm in range(G):
                for t in range(T):
                    step(("rmul", c, gm, t), r_part, c, gm, t)
                    step(("rscale", c, gm, t), r_scale, c, gm, t)
                step(("radd", c, gm), r_add, c, gm)
                step(("rq", "r", c, gm), right_quant, "r", c, gm)
            for j in range(J):
                step(("zmul", c, j), z_mul, c, j)
                step(("zadd", c, j), z_add, c, j)
            for jp in range(4):
                step(("zact", c, jp), z_act, c, jp)
                step(("zbias", c, jp), z_bias, c, jp)
                step(("zout", c, jp), z_out, c, jp)
        with tc.manual_schedule():
            for step_no in ORDER:
                fn, args = todo[step_no]
                fn(*args)
